import numpy as np
import ml_dtypes


def mxq(x, axis, fmt="e4m3"):
    dtype, down = {"e4m3": (ml_dtypes.float8_e4m3fn, 7), "e5m2": (ml_dtypes.float8_e5m2, 14)}[fmt]
    v = np.moveaxis(np.asarray(x, np.float32).astype(ml_dtypes.bfloat16).astype(np.float64), axis, -1)
    blocks = v.reshape(v.shape[:-1] + (-1, 32))
    amax = np.abs(blocks).max(-1, keepdims=True)
    byte = np.maximum(np.where(amax > 0, np.frexp(amax)[1] - 1 + 127, 0) - down, 1)
    scale = np.exp2(byte - 127.0)
    codes = (blocks / scale).astype(np.float32).astype(dtype).astype(np.float64)
    return np.moveaxis((codes * scale).reshape(v.shape), -1, axis)


WIDE = False


def mx_kscale(k):
    if not WIDE:
        return np.ones(k)
    levels = np.array([10, -10, 5, -5, 0])
    if k % 512:
        return np.exp2(np.random.permutation(np.resize(levels, k // 32))).repeat(32)
    a = np.empty((k // 512, 16))
    for p in range(k // 512):
        a[p, :8] = np.random.permutation(np.resize(levels, 8))
        for g in range(8):
            far = levels[np.abs(levels - a[p, g]) >= 10]
            a[p, g + 8] = far[np.random.randint(len(far))]
    return np.exp2(a.ravel()).repeat(32)


def f64(x):
    return np.asarray(x).astype(np.float64)


def striped(idx):
    return np.tile(idx.reshape(-1, 16).T, (8, 1)).astype(np.uint16)


def unstriped(offs):
    return offs[:16].T.reshape(-1).astype(np.int64)


def pack_weight(w):
    k, n = w.shape
    w = f64(np.asarray(w, np.float32).astype(ml_dtypes.bfloat16)).reshape(k // 32, 32, n)
    amax = np.abs(w).max(1)
    byte = np.clip(np.where(amax > 0, np.frexp(amax)[1] - 1 + 127 - 7, 1), 1, 254)
    scaled = (w * np.exp2(127.0 - byte)[:, None, :]).reshape(k, n).astype(np.float32)
    words = np.ascontiguousarray(scaled.reshape(k // 512, 128, 4, n).transpose(0, 1, 3, 2)).astype(ml_dtypes.float8_e4m3fn).view(np.uint8)
    return words, np.ascontiguousarray(byte.astype(np.uint8).reshape(k // 512, 16, n))


def unpack_weight(words, scales):
    g, p, n, _ = words.shape
    vals = np.ascontiguousarray(words).view(ml_dtypes.float8_e4m3fn).astype(np.float64) * np.repeat(np.exp2(scales.astype(np.float64) - 127.0), 8, axis=1)[..., None]
    return vals.transpose(0, 1, 3, 2).reshape(g * 512, n)


K, T, S, N, V, W = 512, 2048, 512, 128, 512, 2048
P = 2 ** 7


def setup_inputs():
    n = np.random.standard_normal
    s = mx_kscale(K)[:, None]
    c = mx_kscale(S)
    packed_xT = pack_weight(n((K, T)) * s)
    packed_eT = pack_weight(n((K, W)) / np.sqrt(K) / s)
    return {
        "x_words": packed_xT[0],
        "x_scales": packed_xT[1],
        "e_words": packed_eT[0],
        "e_scales": packed_eT[1],
        "half": (np.tile(np.random.uniform(0.3, 1.0, W), (P, 1))).astype(np.float32),
        "own": (-np.random.uniform(0.3, 1.0, (S, 1))).astype(np.float32),
        "wgt": (np.random.uniform(0.5, 1.0, (S, 1)) * c[:, None]).astype(np.float32),
        "dual": (n((S, N)) / np.sqrt(S) / c[:, None]).astype(np.float32),
        "bias": (0.5 * n((N, 1))).astype(np.float32),
        "offs": striped(np.random.permutation(T)[:S]),
        "qry": striped(np.random.permutation(W)[:V]),
    }


def reference(x_words, x_scales, e_words, e_scales, half, own, wgt, dual, bias, offs, qry):
    xq = unpack_weight(x_words, x_scales)[:, unstriped(offs)]
    e_qry = unpack_weight(e_words, e_scales)[:, unstriped(qry)]
    ee = np.exp(0.5 * (xq.T @ e_qry) + f64(own) - (f64(half)[:1][:, unstriped(qry)]))
    a = f64(wgt) * ee
    return np.tanh((mxq(f64(dual), 0, "e4m3").T @ mxq(a, 0, "e4m3")) + f64(bias))

@@ -1,0 +1,181 @@
+from contextlib import ExitStack
+
+import concourse.mybir as mybir
+
+K, T, S, N, V, W = 512, 2048, 512, 128, 512, 2048
+FLOPS = 2 * K * S * V + 2 * S * N * V
+BYTES = 2 * (K * T + K * T // 32) + 4 * (W + 2 * S + S * N + N + N * V) + 2 * 128 * (S + V) // 16
+
+F32 = mybir.dt.float32
+BF16 = mybir.dt.bfloat16
+I32 = mybir.dt.int32
+U32 = mybir.dt.uint32
+U16 = mybir.dt.uint16
+U8 = mybir.dt.uint8
+FP8X4 = mybir.dt.float8_e4m3fn_x4
+ACT = mybir.ActivationFunctionType
+ALU = mybir.AluOpType
+
+P = 128
+PACK = 4
+CHUNK = 128
+E_PLANE = 4
+HALF_ROW = 16
+TINY = 2.0 ** -126
+
+
+def tile_picked_ykrr_bias_p_kernel(
+    tc, x_words, x_scales, e_words, e_scales, half, own, wgt, dual, bias, offs, qry, out
+):
+    nc = tc.nc
+    with ExitStack() as ctx:
+        pool = ctx.enter_context(tc.tile_pool(name="keep", bufs=1))
+        psum = ctx.enter_context(tc.psum_pool(name="psum", bufs=1))
+
+        offs_t = pool.tile([P, S // 16], U16, name="offs_t")
+        qry_t = pool.tile([P, V // 16], U16, name="qry_t")
+        xs_win = pool.tile([P, T], U8, name="xs_win", align_bytes=64)
+        es_win = pool.tile([P, W], U8, name="es_win", tag="es_bytes", align_bytes=64)
+        half_win = pool.tile([P, W], F32, name="half_win", align_bytes=64)
+        own_t = pool.tile([P, PACK], F32, name="own_t")
+        wgt_t = pool.tile([P, PACK], F32, name="wgt_t")
+        bias_t = pool.tile([P, 1], F32, name="bias_t")
+        dual_t = pool.tile([P, PACK, N], F32, name="dual_t", align_bytes=64)
+        ident = pool.tile([P, P], F32, name="ident", align_bytes=64)
+
+        seed = pool.tile([P, 1], F32, name="seed")
+        nc.gpsimd.memset(seed[:], 1.0)
+        warm_ln = pool.tile([P, 1], F32, name="warm_ln")
+        nc.scalar.activation(warm_ln[:], seed[:], ACT.Ln)
+
+        nc.gpsimd.memset(xs_win[:].bitcast(I32), 0)
+        for side, tag in enumerate(("xw_bytes", "ew_bytes")):
+            blank = pool.tile([P, P // 2], F32, name=f"blank{side}", tag=tag, align_bytes=64)
+            nc.gpsimd.memset(blank[:], 0.0)
+            nc.gpsimd.affine_select(
+                out=ident[:, side * (P // 2) : (side + 1) * (P // 2)],
+                in_=blank[:],
+                compare_op=ALU.not_equal,
+                fill=1.0,
+                base=-side * (P // 2),
+                pattern=[[-1, P // 2]],
+                channel_multiplier=1,
+            )
+        xw_win = pool.tile([P, T], U32, name="xw_win", tag="xw_bytes", align_bytes=64)
+        ew_win = pool.tile([P, W], U32, name="ew_win", tag="ew_bytes", align_bytes=64)
+        nc.vector.memset(half_win[:], 0.0)
+        nc.vector.memset(es_win[:].bitcast(I32), 0)
+
+        nc.sync.dma_start(offs_t[:], offs)
+        for q in range(4):
+            nc.sync.dma_start(xs_win[32 * q : 32 * q + 4, :].bitcast(I32), x_scales[0, 4 * q : 4 * q + 4, :].bitcast(I32))
+        nc.sync.dma_start(qry_t[:], qry)
+        nc.sync.dma_start(wgt_t[:], wgt.rearrange("(p j) o -> p (j o)", j=PACK))
+        nc.sync.dma_start(xw_win[:].bitcast(I32), x_words[0].rearrange("p n t -> p (n t)").bitcast(I32))
+        nc.sync.dma_start(ew_win[:].bitcast(I32), e_words[0].rearrange("p n t -> p (n t)").bitcast(I32))
+        nc.scalar.dma_start(half_win[HALF_ROW : HALF_ROW + 1, :], half[0:1, :])
+        for q in range(4):
+            nc.scalar.dma_start(
+                es_win[32 * q + E_PLANE : 32 * q + E_PLANE + 4, :].bitcast(I32), e_scales[0, 4 * q : 4 * q + 4, :].bitcast(I32)
+            )
+        nc.gpsimd.dma_start(own_t[:], own.rearrange("(p j) o -> p (j o)", j=PACK))
+        nc.gpsimd.dma_start(dual_t[:], dual.rearrange("(p j) m -> p j m", j=PACK))
+        nc.gpsimd.dma_start(bias_t[:], bias)
+
+        mag = pool.tile([P, PACK], F32, name="mag")
+        sgn = pool.tile([P, PACK], F32, name="sgn")
+        log_mag = pool.tile([P, PACK], F32, name="log_mag")
+        own2 = pool.tile([P, PACK], F32, name="own2")
+        row2 = pool.tile([P, PACK], F32, name="row2")
+        nc.vector.scalar_tensor_tensor(mag[:], wgt_t[:], -1.0, wgt_t[:], ALU.mult, ALU.max)
+        nc.scalar.activation(log_mag[:], mag[:], ACT.Ln, bias=TINY)
+        nc.scalar.activation(sgn[:], wgt_t[:], ACT.Sign, bias=TINY)
+        nc.scalar.activation(own2[:], own_t[:], ACT.Copy, scale=2.0)
+        for j in range(PACK):
+            nc.scalar.activation(row2[:, j : j + 1], log_mag[:, j : j + 1], ACT.Identity, scale=2.0, bias=own2[:, j : j + 1])
+
+        xs_picked = pool.tile([P, S], U8, name="xs_picked", align_bytes=64)
+        xs_dealt = pool.tile([P, PACK, P], U8, name="xs_dealt", align_bytes=64)
+        xw_dealt = pool.tile([P, PACK, P], U32, name="xw_dealt", align_bytes=64)
+        half_picked = pool.tile([P, V], F32, name="half_picked", align_bytes=64)
+        es_picked = pool.tile([P, V], U8, name="es_picked", align_bytes=64)
+        nc.vector.tensor_copy(xs_picked[:], xs_win[:].indirect(offs_t[:]))
+        nc.vector.tensor_copy(half_picked[:], half_win[:].indirect(qry_t[:]))
+        nc.vector.tensor_copy(xs_dealt[:], xs_picked[:].rearrange("p (m j) -> p j m", j=PACK))
+        nc.vector.tensor_copy(xw_dealt[:].rearrange("p j m -> p m j"), xw_win[:].indirect(offs_t[:]))
+        nc.vector.tensor_copy(es_picked[:], es_win[:].indirect(qry_t[:]))
+
+        turned = psum.tile([P, V // P, P], F32, name="turned")
+        for c in range(V // P):
+            nc.tensor.transpose(turned[:, c, :], half_picked[:, c * P : (c + 1) * P], ident[:])
+        half_col = pool.tile([P, V // P], F32, name="half_col")
+        nc.scalar.activation(half_col[:], turned[:, :, HALF_ROW], ACT.Copy, scale=2.0)
+        spread = psum.tile([P, V], F32, name="spread")
+        for c in range(V // P):
+            nc.tensor.transpose(spread[:, c * P : (c + 1) * P], half_col[:, c : c + 1].to_broadcast([P, P]), ident[:])
+        half2 = pool.tile([P, V], F32, name="half2", align_bytes=64)
+        nc.scalar.copy(half2[:], spread[:])
+        warm = pool.tile([P, 1], F32, name="warm")
+        nc.scalar.activation(warm[:], row2[:, 3:4], ACT.Exp, scale=0.0)
+
+        dual_bf = pool.tile([P, N, PACK], BF16, name="dual_bf", align_bytes=64)
+        for j in range(PACK):
+            nc.scalar.activation(dual_bf[:, :, j], dual_t[:, j, :], ACT.Copy, scale=sgn[:, j : j + 1])
+        dual_codes = pool.tile([P, N], U32, name="dual_codes", align_bytes=64)
+        dual_scales = pool.tile([P, N], U8, name="dual_scales", align_bytes=64)
+
+        ew_picked = []
+        for h in range(2):
+            piece = pool.tile([P, V // 2], U32, name=f"ew_picked{h}", tag=("es_bytes" if h == 0 else "ew_late"), align_bytes=64)
+            nc.vector.tensor_copy(piece[:], ew_win[:].indirect(qry_t[:, h * 16 : (h + 1) * 16]))
+            ew_picked.append(piece)
+
+        chunks = V // CHUNK
+        a_bf = []
+        for c in range(chunks):
+            cols = slice(c * CHUNK, (c + 1) * CHUNK)
+            dots = psum.tile([P, PACK, CHUNK], F32, name=f"dots{c}")
+            moving = ew_picked[c // 2][:, (c % 2) * CHUNK : (c % 2 + 1) * CHUNK]
+            for j in range(PACK):
+                nc.tensor.matmul_mx(
+                    out=dots[:, j, :],
+                    lhsT=xw_dealt[:, j, :].bitcast(FP8X4),
+                    lhsT_scale=xs_dealt[:, j, :],
+                    rhs=moving.bitcast(FP8X4),
+                    rhs_scale=es_picked[E_PLANE:P, cols],
+                    start=True,
+                    stop=True,
+                )
+            expo2 = pool.tile([P, PACK, CHUNK], F32, name=f"expo2_{c}", align_bytes=64)
+            for j in range(PACK):
+                nc.vector.scalar_tensor_tensor(
+                    expo2[:, j, :], dots[:, j, :], row2[:, j : j + 1], half2[:, cols], ALU.add, ALU.subtract
+                )
+            rounded = pool.tile([P, CHUNK, PACK], BF16, name=f"a_bf{c}", align_bytes=64)
+            nc.scalar.activation(
+                rounded[:].rearrange("p (g i) j -> p g j i", i=4),
+                expo2[:].rearrange("p j (g i) -> p g j i", i=4),
+                ACT.Exp,
+                scale=0.5,
+            )
+            a_bf.append(rounded)
+
+        nc.vector.quantize_mx(out=dual_codes[:].bitcast(FP8X4), scales=dual_scales[:], in_=dual_bf[:].rearrange("p m j -> p (m j)"))
+        for c in range(chunks):
+            cols = slice(c * CHUNK, (c + 1) * CHUNK)
+            a_codes = pool.tile([P, CHUNK], U32, name=f"a_codes{c}", align_bytes=64)
+            a_scales = pool.tile([P, CHUNK], U8, name=f"a_scales{c}", align_bytes=64)
+            nc.vector.quantize_mx(out=a_codes[:].bitcast(FP8X4), scales=a_scales[:], in_=a_bf[c][:].rearrange("p v j -> p (v j)"))
+            acc = psum.tile([P, CHUNK], F32, name=f"acc{c % 2}")
+            nc.tensor.matmul_mx(
+                out=acc[:],
+                lhsT=dual_codes[:].bitcast(FP8X4),
+                lhsT_scale=dual_scales[:],
+                rhs=a_codes[:].bitcast(FP8X4),
+                rhs_scale=a_scales[:],
+                start=True,
+                stop=True,
+            )
+            result = pool.tile([P, CHUNK], F32, name=f"result{c}", align_bytes=64)
+            nc.scalar.activation(result[:], acc[:], ACT.Tanh, bias=bias_t[:])
+            nc.sync.dma_start(out[:, cols], result[:])

@@ -1,6 +1,7 @@
 from contextlib import ExitStack
 
 import concourse.mybir as mybir
+from concourse.masks import make_identity
 
 K, T, S, N, V, W = 512, 2048, 512, 128, 512, 2048
 FLOPS = 2 * K * S * V + 2 * S * N * V
@@ -34,37 +35,19 @@ def tile_picked_ykrr_bias_p_kernel(
 
         offs_t = pool.tile([P, S // 16], U16, name="offs_t")
         qry_t = pool.tile([P, V // 16], U16, name="qry_t")
-        xs_win = pool.tile([P, T], U8, name="xs_win", align_bytes=64)
+        xs_win = pool.tile([P, T], U8, name="xs_win", tag="xs_bytes", align_bytes=64)
         es_win = pool.tile([P, W], U8, name="es_win", tag="es_bytes", align_bytes=64)
         half_win = pool.tile([P, W], F32, name="half_win", align_bytes=64)
-        own_t = pool.tile([P, PACK], F32, name="own_t")
-        wgt_t = pool.tile([P, PACK], F32, name="wgt_t")
-        bias_t = pool.tile([P, 1], F32, name="bias_t")
-        dual_t = pool.tile([P, PACK, N], F32, name="dual_t", align_bytes=64)
+        wgt_t = pool.tile([P, PACK], F32, name="wgt_t", tag="ew_bytes", align_bytes=64)
         ident = pool.tile([P, P], F32, name="ident", align_bytes=64)
 
-        seed = pool.tile([P, 1], F32, name="seed")
-        nc.gpsimd.memset(seed[:], 1.0)
-        warm_ln = pool.tile([P, 1], F32, name="warm_ln")
-        nc.scalar.activation(warm_ln[:], seed[:], ACT.Ln)
-
-        nc.gpsimd.memset(xs_win[:].bitcast(I32), 0)
-        for side, tag in enumerate(("xw_bytes", "ew_bytes")):
-            blank = pool.tile([P, P // 2], F32, name=f"blank{side}", tag=tag, align_bytes=64)
-            nc.gpsimd.memset(blank[:], 0.0)
-            nc.gpsimd.affine_select(
-                out=ident[:, side * (P // 2) : (side + 1) * (P // 2)],
-                in_=blank[:],
-                compare_op=ALU.not_equal,
-                fill=1.0,
-                base=-side * (P // 2),
-                pattern=[[-1, P // 2]],
-                channel_multiplier=1,
-            )
-        xw_win = pool.tile([P, T], U32, name="xw_win", tag="xw_bytes", align_bytes=64)
-        ew_win = pool.tile([P, W], U32, name="ew_win", tag="ew_bytes", align_bytes=64)
-        nc.vector.memset(half_win[:], 0.0)
+        make_identity(nc, ident[:])
+        zero = pool.tile([P, 1], F32, name="zero", tag="xw_bytes", align_bytes=64)
+        nc.vector.memset(zero[:], 0.0)
+        nc.vector.memset(xs_win[:].bitcast(I32), 0)
+        nc.vector.tensor_copy(half_win[:], zero[:].to_broadcast([P, W]))
         nc.vector.memset(es_win[:].bitcast(I32), 0)
+        xw_win = pool.tile([P, T], U32, name="xw_win", tag="xw_bytes", align_bytes=64)
 
         nc.sync.dma_start(offs_t[:], offs)
         for q in range(4):
@@ -72,37 +55,41 @@ def tile_picked_ykrr_bias_p_kernel(
         nc.sync.dma_start(qry_t[:], qry)
         nc.sync.dma_start(wgt_t[:], wgt.rearrange("(p j) o -> p (j o)", j=PACK))
         nc.sync.dma_start(xw_win[:].bitcast(I32), x_words[0].rearrange("p n t -> p (n t)").bitcast(I32))
-        nc.sync.dma_start(ew_win[:].bitcast(I32), e_words[0].rearrange("p n t -> p (n t)").bitcast(I32))
         nc.scalar.dma_start(half_win[HALF_ROW : HALF_ROW + 1, :], half[0:1, :])
         for q in range(4):
             nc.scalar.dma_start(
                 es_win[32 * q + E_PLANE : 32 * q + E_PLANE + 4, :].bitcast(I32), e_scales[0, 4 * q : 4 * q + 4, :].bitcast(I32)
             )
-        nc.gpsimd.dma_start(own_t[:], own.rearrange("(p j) o -> p (j o)", j=PACK))
-        nc.gpsimd.dma_start(dual_t[:], dual.rearrange("(p j) m -> p j m", j=PACK))
-        nc.gpsimd.dma_start(bias_t[:], bias)
 
         mag = pool.tile([P, PACK], F32, name="mag")
+        step2 = pool.tile([P, PACK], F32, name="step2", tag="own_bytes")
         sgn = pool.tile([P, PACK], F32, name="sgn")
         log_mag = pool.tile([P, PACK], F32, name="log_mag")
         own2 = pool.tile([P, PACK], F32, name="own2")
         row2 = pool.tile([P, PACK], F32, name="row2")
+        nc.vector.tensor_scalar(step2[:], wgt_t[:], 0.0, 2.0, ALU.is_ge, ALU.mult)
         nc.vector.scalar_tensor_tensor(mag[:], wgt_t[:], -1.0, wgt_t[:], ALU.mult, ALU.max)
+        nc.vector.tensor_scalar(sgn[:], step2[:], -1.0, None, ALU.add)
+        ew_win = pool.tile([P, W], U32, name="ew_win", tag="ew_bytes", align_bytes=64)
+        nc.sync.dma_start(ew_win[:].bitcast(I32), e_words[0].rearrange("p n t -> p (n t)").bitcast(I32))
+        own_t = pool.tile([P, PACK], F32, name="own_t", tag="own_bytes")
+        nc.scalar.dma_start(own_t[:], own.rearrange("(p j) o -> p (j o)", j=PACK))
         nc.scalar.activation(log_mag[:], mag[:], ACT.Ln, bias=TINY)
-        nc.scalar.activation(sgn[:], wgt_t[:], ACT.Sign, bias=TINY)
+        warm = pool.tile([P, 1], F32, name="warm")
+        nc.scalar.activation(warm[:], log_mag[:, 0:1], ACT.Exp, scale=0.0)
         nc.scalar.activation(own2[:], own_t[:], ACT.Copy, scale=2.0)
         for j in range(PACK):
             nc.scalar.activation(row2[:, j : j + 1], log_mag[:, j : j + 1], ACT.Identity, scale=2.0, bias=own2[:, j : j + 1])
 
-        xs_picked = pool.tile([P, S], U8, name="xs_picked", align_bytes=64)
+        xs_picked = pool.tile([P, S], U8, name="xs_picked", tag="bias_bytes", align_bytes=64)
         xs_dealt = pool.tile([P, PACK, P], U8, name="xs_dealt", align_bytes=64)
         xw_dealt = pool.tile([P, PACK, P], U32, name="xw_dealt", align_bytes=64)
         half_picked = pool.tile([P, V], F32, name="half_picked", align_bytes=64)
-        es_picked = pool.tile([P, V], U8, name="es_picked", align_bytes=64)
         nc.vector.tensor_copy(xs_picked[:], xs_win[:].indirect(offs_t[:]))
         nc.vector.tensor_copy(half_picked[:], half_win[:].indirect(qry_t[:]))
         nc.vector.tensor_copy(xs_dealt[:], xs_picked[:].rearrange("p (m j) -> p j m", j=PACK))
         nc.vector.tensor_copy(xw_dealt[:].rearrange("p j m -> p m j"), xw_win[:].indirect(offs_t[:]))
+        es_picked = pool.tile([P, V], U8, name="es_picked", tag="xw_bytes", align_bytes=64)
         nc.vector.tensor_copy(es_picked[:], es_win[:].indirect(qry_t[:]))
 
         turned = psum.tile([P, V // P, P], F32, name="turned")
@@ -115,9 +102,11 @@ def tile_picked_ykrr_bias_p_kernel(
             nc.tensor.transpose(spread[:, c * P : (c + 1) * P], half_col[:, c : c + 1].to_broadcast([P, P]), ident[:])
         half2 = pool.tile([P, V], F32, name="half2", align_bytes=64)
         nc.scalar.copy(half2[:], spread[:])
-        warm = pool.tile([P, 1], F32, name="warm")
-        nc.scalar.activation(warm[:], row2[:, 3:4], ACT.Exp, scale=0.0)
 
+        dual_t = pool.tile([P, PACK, N], F32, name="dual_t", tag="xs_bytes", align_bytes=64)
+        nc.sync.dma_start(dual_t[:], dual.rearrange("(p j) m -> p j m", j=PACK))
+        bias_t = pool.tile([P, 1], F32, name="bias_t", tag="bias_bytes", align_bytes=64)
+        nc.sync.dma_start(bias_t[:], bias)
         dual_bf = pool.tile([P, N, PACK], BF16, name="dual_bf", align_bytes=64)
         for j in range(PACK):
             nc.scalar.activation(dual_bf[:, :, j], dual_t[:, j, :], ACT.Copy, scale=sgn[:, j : j + 1])

@@ -35,10 +35,10 @@ def tile_picked_ykrr_bias_p_kernel(
 
         offs_t = pool.tile([P, S // 16], U16, name="offs_t")
         qry_t = pool.tile([P, V // 16], U16, name="qry_t")
-        xs_win = pool.tile([P, T], U8, name="xs_win", tag="xs_bytes", align_bytes=64)
+        xs_win = pool.tile([P, T], U8, name="xs_win", tag="ew_bytes", align_bytes=64)
         es_win = pool.tile([P, W], U8, name="es_win", tag="es_bytes", align_bytes=64)
-        half_win = pool.tile([P, W], F32, name="half_win", align_bytes=64)
-        wgt_t = pool.tile([P, PACK], F32, name="wgt_t", tag="ew_bytes", align_bytes=64)
+        half_win = pool.tile([P, W], F32, name="half_win", tag="bias_bytes", align_bytes=64)
+        wgt_t = pool.tile([P, PACK], F32, name="wgt_t")
         ident = pool.tile([P, P], F32, name="ident", align_bytes=64)
 
         make_identity(nc, ident[:])
@@ -49,43 +49,44 @@ def tile_picked_ykrr_bias_p_kernel(
         nc.vector.memset(es_win[:].bitcast(I32), 0)
         xw_win = pool.tile([P, T], U32, name="xw_win", tag="xw_bytes", align_bytes=64)
 
+        own_t = pool.tile([P, PACK], F32, name="own_t")
         nc.sync.dma_start(offs_t[:], offs)
         for q in range(4):
-            nc.sync.dma_start(xs_win[32 * q : 32 * q + 4, :].bitcast(I32), x_scales[0, 4 * q : 4 * q + 4, :].bitcast(I32))
+            queue = nc.sync if q % 2 == 0 else nc.scalar
+            queue.dma_start(xs_win[32 * q : 32 * q + 4, :].bitcast(I32), x_scales[0, 4 * q : 4 * q + 4, :].bitcast(I32))
         nc.sync.dma_start(qry_t[:], qry)
         nc.sync.dma_start(wgt_t[:], wgt.rearrange("(p j) o -> p (j o)", j=PACK))
+        nc.sync.dma_start(own_t[:], own.rearrange("(p j) o -> p (j o)", j=PACK))
+        nc.sync.dma_start(half_win[HALF_ROW : HALF_ROW + 1, :], half[0:1, :])
         nc.sync.dma_start(xw_win[:].bitcast(I32), x_words[0].rearrange("p n t -> p (n t)").bitcast(I32))
-        nc.scalar.dma_start(half_win[HALF_ROW : HALF_ROW + 1, :], half[0:1, :])
         for q in range(4):
-            nc.scalar.dma_start(
+            nc.sync.dma_start(
                 es_win[32 * q + E_PLANE : 32 * q + E_PLANE + 4, :].bitcast(I32), e_scales[0, 4 * q : 4 * q + 4, :].bitcast(I32)
             )
 
         mag = pool.tile([P, PACK], F32, name="mag")
-        step2 = pool.tile([P, PACK], F32, name="step2", tag="own_bytes")
+        step2 = pool.tile([P, PACK], F32, name="step2")
         sgn = pool.tile([P, PACK], F32, name="sgn")
         log_mag = pool.tile([P, PACK], F32, name="log_mag")
-        own2 = pool.tile([P, PACK], F32, name="own2")
+        log_mag2 = pool.tile([P, PACK], F32, name="log_mag2")
         row2 = pool.tile([P, PACK], F32, name="row2")
-        nc.vector.tensor_scalar(step2[:], wgt_t[:], 0.0, 2.0, ALU.is_ge, ALU.mult)
         nc.vector.scalar_tensor_tensor(mag[:], wgt_t[:], -1.0, wgt_t[:], ALU.mult, ALU.max)
-        nc.vector.tensor_scalar(sgn[:], step2[:], -1.0, None, ALU.add)
-        ew_win = pool.tile([P, W], U32, name="ew_win", tag="ew_bytes", align_bytes=64)
-        nc.sync.dma_start(ew_win[:].bitcast(I32), e_words[0].rearrange("p n t -> p (n t)").bitcast(I32))
-        own_t = pool.tile([P, PACK], F32, name="own_t", tag="own_bytes")
-        nc.scalar.dma_start(own_t[:], own.rearrange("(p j) o -> p (j o)", j=PACK))
+        nc.gpsimd.tensor_scalar(step2[:], wgt_t[:], 0.0, 2.0, ALU.is_ge, ALU.mult)
+        nc.gpsimd.tensor_scalar(sgn[:], step2[:], 1.0, -1.0, ALU.mult, ALU.add)
         nc.scalar.activation(log_mag[:], mag[:], ACT.Ln, bias=TINY)
-        warm = pool.tile([P, 1], F32, name="warm")
-        nc.scalar.activation(warm[:], log_mag[:, 0:1], ACT.Exp, scale=0.0)
-        nc.scalar.activation(own2[:], own_t[:], ACT.Copy, scale=2.0)
+        nc.scalar.activation(log_mag2[:], log_mag[:], ACT.Copy, scale=2.0)
         for j in range(PACK):
-            nc.scalar.activation(row2[:, j : j + 1], log_mag[:, j : j + 1], ACT.Identity, scale=2.0, bias=own2[:, j : j + 1])
+            nc.scalar.activation(row2[:, j : j + 1], own_t[:, j : j + 1], ACT.Identity, scale=2.0, bias=log_mag2[:, j : j + 1])
+        warm = pool.tile([P, 1], F32, name="warm")
+        nc.scalar.activation(warm[:], row2[:, PACK - 1 : PACK], ACT.Exp, scale=0.0)
 
-        xs_picked = pool.tile([P, S], U8, name="xs_picked", tag="bias_bytes", align_bytes=64)
+        xs_picked = pool.tile([P, S], U8, name="xs_picked", tag="dual_bytes", align_bytes=64)
         xs_dealt = pool.tile([P, PACK, P], U8, name="xs_dealt", align_bytes=64)
         xw_dealt = pool.tile([P, PACK, P], U32, name="xw_dealt", align_bytes=64)
         half_picked = pool.tile([P, V], F32, name="half_picked", align_bytes=64)
         nc.vector.tensor_copy(xs_picked[:], xs_win[:].indirect(offs_t[:]))
+        ew_win = pool.tile([P, W], U32, name="ew_win", tag="ew_bytes", align_bytes=64)
+        nc.sync.dma_start(ew_win[:].bitcast(I32), e_words[0].rearrange("p n t -> p (n t)").bitcast(I32))
         nc.vector.tensor_copy(half_picked[:], half_win[:].indirect(qry_t[:]))
         nc.vector.tensor_copy(xs_dealt[:], xs_picked[:].rearrange("p (m j) -> p j m", j=PACK))
         nc.vector.tensor_copy(xw_dealt[:].rearrange("p j m -> p m j"), xw_win[:].indirect(offs_t[:]))
@@ -96,20 +97,23 @@ def tile_picked_ykrr_bias_p_kernel(
         for c in range(V // P):
             nc.tensor.transpose(turned[:, c, :], half_picked[:, c * P : (c + 1) * P], ident[:])
         half_col = pool.tile([P, V // P], F32, name="half_col")
-        nc.scalar.activation(half_col[:], turned[:, :, HALF_ROW], ACT.Copy, scale=2.0)
+        nc.scalar.activation(half_col[:], turned[:, :, HALF_ROW], ACT.Copy, scale=-2.0)
         spread = psum.tile([P, V], F32, name="spread")
         for c in range(V // P):
             nc.tensor.transpose(spread[:, c * P : (c + 1) * P], half_col[:, c : c + 1].to_broadcast([P, P]), ident[:])
-        half2 = pool.tile([P, V], F32, name="half2", align_bytes=64)
-        nc.scalar.copy(half2[:], spread[:])
+        norms2 = []
+        for h in range(2):
+            piece = pool.tile([P, PACK, V // 2], F32, name=f"norms2_{h}", align_bytes=64)
+            for j in range(PACK):
+                nc.scalar.activation(
+                    piece[:, j, :], spread[:, h * (V // 2) : (h + 1) * (V // 2)], ACT.Identity, bias=row2[:, j : j + 1]
+                )
+            norms2.append(piece)
 
-        dual_t = pool.tile([P, PACK, N], F32, name="dual_t", tag="xs_bytes", align_bytes=64)
+        dual_t = pool.tile([P, PACK, N], F32, name="dual_t", tag="dual_bytes", align_bytes=64)
         nc.sync.dma_start(dual_t[:], dual.rearrange("(p j) m -> p j m", j=PACK))
         bias_t = pool.tile([P, 1], F32, name="bias_t", tag="bias_bytes", align_bytes=64)
         nc.sync.dma_start(bias_t[:], bias)
-        dual_bf = pool.tile([P, N, PACK], BF16, name="dual_bf", align_bytes=64)
-        for j in range(PACK):
-            nc.scalar.activation(dual_bf[:, :, j], dual_t[:, j, :], ACT.Copy, scale=sgn[:, j : j + 1])
         dual_codes = pool.tile([P, N], U32, name="dual_codes", align_bytes=64)
         dual_scales = pool.tile([P, N], U8, name="dual_scales", align_bytes=64)
 
@@ -119,43 +123,45 @@ def tile_picked_ykrr_bias_p_kernel(
             nc.vector.tensor_copy(piece[:], ew_win[:].indirect(qry_t[:, h * 16 : (h + 1) * 16]))
             ew_picked.append(piece)
 
-        chunks = V // CHUNK
-        a_bf = []
-        for c in range(chunks):
-            cols = slice(c * CHUNK, (c + 1) * CHUNK)
+        dual_bf = pool.tile([P, N, PACK], BF16, name="dual_bf", tag="ew_bytes", align_bytes=64)
+        nc.gpsimd.tensor_tensor(
+            dual_bf[:], dual_t[:].rearrange("p j m -> p m j"), sgn[:].unsqueeze(1).to_broadcast([P, N, PACK]), ALU.mult
+        )
+
+        spans = []
+        for c in range(V // CHUNK):
             dots = psum.tile([P, PACK, CHUNK], F32, name=f"dots{c}")
-            moving = ew_picked[c // 2][:, (c % 2) * CHUNK : (c % 2 + 1) * CHUNK]
+            h, lo = divmod(c * CHUNK, V // 2)
             for j in range(PACK):
                 nc.tensor.matmul_mx(
                     out=dots[:, j, :],
                     lhsT=xw_dealt[:, j, :].bitcast(FP8X4),
                     lhsT_scale=xs_dealt[:, j, :],
-                    rhs=moving.bitcast(FP8X4),
-                    rhs_scale=es_picked[E_PLANE:P, cols],
+                    rhs=ew_picked[h][:, lo : lo + CHUNK].bitcast(FP8X4),
+                    rhs_scale=es_picked[E_PLANE:P, c * CHUNK : (c + 1) * CHUNK],
                     start=True,
                     stop=True,
                 )
-            expo2 = pool.tile([P, PACK, CHUNK], F32, name=f"expo2_{c}", align_bytes=64)
-            for j in range(PACK):
-                nc.vector.scalar_tensor_tensor(
-                    expo2[:, j, :], dots[:, j, :], row2[:, j : j + 1], half2[:, cols], ALU.add, ALU.subtract
+            width = CHUNK if c < V // CHUNK - 1 else CHUNK // 2
+            for at in range(0, CHUNK, width):
+                first = c * CHUNK + at
+                expo2 = pool.tile([P, PACK, width], F32, name=f"expo2_{first}", align_bytes=64)
+                nc.vector.tensor_tensor(expo2[:], dots[:, :, at : at + width], norms2[h][:, :, lo + at : lo + at + width], ALU.add)
+                rounded = pool.tile([P, width, PACK], BF16, name=f"a_bf{first}", align_bytes=64)
+                nc.scalar.activation(
+                    rounded[:].rearrange("p (g i) j -> p g j i", i=4),
+                    expo2[:].rearrange("p j (g i) -> p g j i", i=4),
+                    ACT.Exp,
+                    scale=0.5,
                 )
-            rounded = pool.tile([P, CHUNK, PACK], BF16, name=f"a_bf{c}", align_bytes=64)
-            nc.scalar.activation(
-                rounded[:].rearrange("p (g i) j -> p g j i", i=4),
-                expo2[:].rearrange("p j (g i) -> p g j i", i=4),
-                ACT.Exp,
-                scale=0.5,
-            )
-            a_bf.append(rounded)
+                spans.append((first, width, rounded))
 
         nc.vector.quantize_mx(out=dual_codes[:].bitcast(FP8X4), scales=dual_scales[:], in_=dual_bf[:].rearrange("p m j -> p (m j)"))
-        for c in range(chunks):
-            cols = slice(c * CHUNK, (c + 1) * CHUNK)
-            a_codes = pool.tile([P, CHUNK], U32, name=f"a_codes{c}", align_bytes=64)
-            a_scales = pool.tile([P, CHUNK], U8, name=f"a_scales{c}", align_bytes=64)
-            nc.vector.quantize_mx(out=a_codes[:].bitcast(FP8X4), scales=a_scales[:], in_=a_bf[c][:].rearrange("p v j -> p (v j)"))
-            acc = psum.tile([P, CHUNK], F32, name=f"acc{c % 2}")
+        for n, (first, width, rounded) in enumerate(spans):
+            a_codes = pool.tile([P, width], U32, name=f"a_codes{first}", align_bytes=64)
+            a_scales = pool.tile([P, width], U8, name=f"a_scales{first}", align_bytes=64)
+            nc.vector.quantize_mx(out=a_codes[:].bitcast(FP8X4), scales=a_scales[:], in_=rounded[:].rearrange("p v j -> p (v j)"))
+            acc = psum.tile([P, width], F32, name=f"acc{n}", tag=["acc0", "acc1", "turned", "spread", "dots0"][n])
             nc.tensor.matmul_mx(
                 out=acc[:],
                 lhsT=dual_codes[:].bitcast(FP8X4),
@@ -165,6 +171,6 @@ def tile_picked_ykrr_bias_p_kernel(
                 start=True,
                 stop=True,
             )
-            result = pool.tile([P, CHUNK], F32, name=f"result{c}", align_bytes=64)
+            result = pool.tile([P, width], F32, name=f"result{first}", align_bytes=64)
             nc.scalar.activation(result[:], acc[:], ACT.Tanh, bias=bias_t[:])
-            nc.sync.dma_start(out[:, cols], result[:])
+            nc.sync.dma_start(out[:, first : first + width], result[:])

@@ -21,7 +21,8 @@ P = 128
 PACK = 4
 CHUNK = 128
 E_PLANE = 4
-HALF_ROW = 16
+HALF_ROW = 127
+FIRST_FILL = 64
 TINY = 2.0 ** -126
 
 
@@ -33,64 +34,53 @@ def tile_picked_ykrr_bias_p_kernel(
         pool = ctx.enter_context(tc.tile_pool(name="keep", bufs=1))
         psum = ctx.enter_context(tc.psum_pool(name="psum", bufs=1))
 
+        held = ctx.enter_context(tc.tile_pool(name="held", bufs=1))
+
         offs_t = pool.tile([P, S // 16], U16, name="offs_t")
         qry_t = pool.tile([P, V // 16], U16, name="qry_t")
-        xs_win = pool.tile([P, T], U8, name="xs_win", tag="ew_bytes", align_bytes=64)
-        es_win = pool.tile([P, W], U8, name="es_win", tag="es_bytes", align_bytes=64)
-        half_win = pool.tile([P, W], F32, name="half_win", tag="bias_bytes", align_bytes=64)
-        wgt_t = pool.tile([P, PACK], F32, name="wgt_t")
-        ident = pool.tile([P, P], F32, name="ident", align_bytes=64)
+        xs_win = pool.tile([P, T], U8, name="xs_win", tag="xs_bytes", align_bytes=64)
+        es_win = pool.tile([P, W], U8, name="es_win", align_bytes=64)
+        half_win = pool.tile([P, W], F32, name="half_win", tag="half_bytes", align_bytes=64)
 
-        make_identity(nc, ident[:])
-        zero = pool.tile([P, 1], F32, name="zero", tag="xw_bytes", align_bytes=64)
-        nc.vector.memset(zero[:], 0.0)
+        zero = held.tile([P, 32], F32, name="zero", offset=480)
+        zero_rest = pool.tile([P, 1], F32, name="zero_rest", tag="ew_bytes", align_bytes=64)
         nc.vector.memset(xs_win[:].bitcast(I32), 0)
-        nc.vector.tensor_copy(half_win[:], zero[:].to_broadcast([P, W]))
+        nc.vector.memset(zero[:], 0.0)
+        nc.vector.memset(zero_rest[:], 0.0)
+        nc.vector.tensor_copy(half_win[:HALF_ROW, :FIRST_FILL], zero[:HALF_ROW, 0:1].to_broadcast([HALF_ROW, FIRST_FILL]))
         nc.vector.memset(es_win[:].bitcast(I32), 0)
-        xw_win = pool.tile([P, T], U32, name="xw_win", tag="xw_bytes", align_bytes=64)
+        nc.vector.tensor_copy(half_win[:HALF_ROW, FIRST_FILL:], zero_rest[:HALF_ROW, :].to_broadcast([HALF_ROW, W - FIRST_FILL]))
+        ident = held.tile([P, P], F32, name="ident", offset=0, align_bytes=64)
+        wgt_t = held.tile([P, PACK], F32, name="wgt_t", offset=512)
+        own_t = held.tile([P, PACK], F32, name="own_t", offset=544)
+        xw_win = held.tile([P, T], U32, name="xw_win", offset=576, align_bytes=64)
+        ew_win = pool.tile([P, W], U32, name="ew_win", tag="ew_bytes", align_bytes=64)
+        make_identity(nc, ident[:])
 
-        own_t = pool.tile([P, PACK], F32, name="own_t")
+        nc.sync.dma_start(qry_t[:], qry)
+        nc.sync.dma_start(half_win[HALF_ROW : HALF_ROW + 1, :], half[0:1, :])
         nc.sync.dma_start(offs_t[:], offs)
         for q in range(4):
             queue = nc.sync if q % 2 == 0 else nc.scalar
             queue.dma_start(xs_win[32 * q : 32 * q + 4, :].bitcast(I32), x_scales[0, 4 * q : 4 * q + 4, :].bitcast(I32))
-        nc.sync.dma_start(qry_t[:], qry)
+        nc.sync.dma_start(xw_win[:].bitcast(I32), x_words[0].rearrange("p n t -> p (n t)").bitcast(I32))
         nc.sync.dma_start(wgt_t[:], wgt.rearrange("(p j) o -> p (j o)", j=PACK))
         nc.sync.dma_start(own_t[:], own.rearrange("(p j) o -> p (j o)", j=PACK))
-        nc.sync.dma_start(half_win[HALF_ROW : HALF_ROW + 1, :], half[0:1, :])
-        nc.sync.dma_start(xw_win[:].bitcast(I32), x_words[0].rearrange("p n t -> p (n t)").bitcast(I32))
         for q in range(4):
             nc.sync.dma_start(
                 es_win[32 * q + E_PLANE : 32 * q + E_PLANE + 4, :].bitcast(I32), e_scales[0, 4 * q : 4 * q + 4, :].bitcast(I32)
             )
+        nc.sync.dma_start(ew_win[:].bitcast(I32), e_words[0].rearrange("p n t -> p (n t)").bitcast(I32))
 
-        mag = pool.tile([P, PACK], F32, name="mag")
-        step2 = pool.tile([P, PACK], F32, name="step2")
-        sgn = pool.tile([P, PACK], F32, name="sgn")
-        log_mag = pool.tile([P, PACK], F32, name="log_mag")
-        log_mag2 = pool.tile([P, PACK], F32, name="log_mag2")
-        row2 = pool.tile([P, PACK], F32, name="row2")
-        nc.vector.scalar_tensor_tensor(mag[:], wgt_t[:], -1.0, wgt_t[:], ALU.mult, ALU.max)
-        nc.gpsimd.tensor_scalar(step2[:], wgt_t[:], 0.0, 2.0, ALU.is_ge, ALU.mult)
-        nc.gpsimd.tensor_scalar(sgn[:], step2[:], 1.0, -1.0, ALU.mult, ALU.add)
-        nc.scalar.activation(log_mag[:], mag[:], ACT.Ln, bias=TINY)
-        nc.scalar.activation(log_mag2[:], log_mag[:], ACT.Copy, scale=2.0)
-        for j in range(PACK):
-            nc.scalar.activation(row2[:, j : j + 1], own_t[:, j : j + 1], ACT.Identity, scale=2.0, bias=log_mag2[:, j : j + 1])
-        warm = pool.tile([P, 1], F32, name="warm")
-        nc.scalar.activation(warm[:], row2[:, PACK - 1 : PACK], ACT.Exp, scale=0.0)
-
-        xs_picked = pool.tile([P, S], U8, name="xs_picked", tag="dual_bytes", align_bytes=64)
+        half_picked = pool.tile([P, V], F32, name="half_picked", align_bytes=64)
+        xs_picked = pool.tile([P, S], U8, name="xs_picked", tag="picked_bytes", align_bytes=64)
         xs_dealt = pool.tile([P, PACK, P], U8, name="xs_dealt", align_bytes=64)
         xw_dealt = pool.tile([P, PACK, P], U32, name="xw_dealt", align_bytes=64)
-        half_picked = pool.tile([P, V], F32, name="half_picked", align_bytes=64)
-        nc.vector.tensor_copy(xs_picked[:], xs_win[:].indirect(offs_t[:]))
-        ew_win = pool.tile([P, W], U32, name="ew_win", tag="ew_bytes", align_bytes=64)
-        nc.sync.dma_start(ew_win[:].bitcast(I32), e_words[0].rearrange("p n t -> p (n t)").bitcast(I32))
         nc.vector.tensor_copy(half_picked[:], half_win[:].indirect(qry_t[:]))
+        nc.vector.tensor_copy(xs_picked[:], xs_win[:].indirect(offs_t[:]))
         nc.vector.tensor_copy(xs_dealt[:], xs_picked[:].rearrange("p (m j) -> p j m", j=PACK))
         nc.vector.tensor_copy(xw_dealt[:].rearrange("p j m -> p m j"), xw_win[:].indirect(offs_t[:]))
-        es_picked = pool.tile([P, V], U8, name="es_picked", tag="xw_bytes", align_bytes=64)
+        es_picked = pool.tile([P, V], U8, name="es_picked", tag="picked_bytes", align_bytes=64)
         nc.vector.tensor_copy(es_picked[:], es_win[:].indirect(qry_t[:]))
 
         turned = psum.tile([P, V // P, P], F32, name="turned")
@@ -101,25 +91,32 @@ def tile_picked_ykrr_bias_p_kernel(
         spread = psum.tile([P, V], F32, name="spread")
         for c in range(V // P):
             nc.tensor.transpose(spread[:, c * P : (c + 1) * P], half_col[:, c : c + 1].to_broadcast([P, P]), ident[:])
-        norms2 = []
-        for h in range(2):
-            piece = pool.tile([P, PACK, V // 2], F32, name=f"norms2_{h}", align_bytes=64)
-            for j in range(PACK):
-                nc.scalar.activation(
-                    piece[:, j, :], spread[:, h * (V // 2) : (h + 1) * (V // 2)], ACT.Identity, bias=row2[:, j : j + 1]
-                )
-            norms2.append(piece)
+        cols2 = pool.tile([P, V], F32, name="cols2", align_bytes=64)
+        nc.scalar.copy(cols2[:], spread[:])
 
-        dual_t = pool.tile([P, PACK, N], F32, name="dual_t", tag="dual_bytes", align_bytes=64)
+        mag = pool.tile([P, PACK], F32, name="mag")
+        step2 = pool.tile([P, PACK], F32, name="step2")
+        sgn = pool.tile([P, PACK], F32, name="sgn")
+        log_mag = pool.tile([P, PACK], F32, name="log_mag")
+        row = pool.tile([P, PACK], F32, name="row")
+        row2 = pool.tile([P, PACK], F32, name="row2")
+        nc.gpsimd.tensor_scalar(step2[:], wgt_t[:], 0.0, 2.0, ALU.is_ge, ALU.mult)
+        nc.gpsimd.tensor_scalar(sgn[:], step2[:], 1.0, -1.0, ALU.mult, ALU.add)
+        nc.gpsimd.tensor_tensor(mag[:], wgt_t[:], sgn[:], ALU.mult)
+        nc.scalar.activation(log_mag[:], mag[:], ACT.Ln, bias=TINY)
+        nc.gpsimd.tensor_tensor(row[:], log_mag[:], own_t[:], ALU.add)
+        nc.gpsimd.tensor_scalar(row2[:], row[:], 2.0, 0.0, ALU.mult, ALU.add)
+
+        dual_t = pool.tile([P, PACK, N], F32, name="dual_t", tag="half_bytes", align_bytes=64)
         nc.sync.dma_start(dual_t[:], dual.rearrange("(p j) m -> p j m", j=PACK))
-        bias_t = pool.tile([P, 1], F32, name="bias_t", tag="bias_bytes", align_bytes=64)
+        bias_t = pool.tile([P, 1], F32, name="bias_t", tag="xs_bytes", align_bytes=64)
         nc.sync.dma_start(bias_t[:], bias)
         dual_codes = pool.tile([P, N], U32, name="dual_codes", align_bytes=64)
         dual_scales = pool.tile([P, N], U8, name="dual_scales", align_bytes=64)
 
         ew_picked = []
         for h in range(2):
-            piece = pool.tile([P, V // 2], U32, name=f"ew_picked{h}", tag=("es_bytes" if h == 0 else "ew_late"), align_bytes=64)
+            piece = pool.tile([P, V // 2], U32, name=f"ew_picked{h}", align_bytes=64)
             nc.vector.tensor_copy(piece[:], ew_win[:].indirect(qry_t[:, h * 16 : (h + 1) * 16]))
             ew_picked.append(piece)
 
@@ -146,7 +143,10 @@ def tile_picked_ykrr_bias_p_kernel(
             for at in range(0, CHUNK, width):
                 first = c * CHUNK + at
                 expo2 = pool.tile([P, PACK, width], F32, name=f"expo2_{first}", align_bytes=64)
-                nc.vector.tensor_tensor(expo2[:], dots[:, :, at : at + width], norms2[h][:, :, lo + at : lo + at + width], ALU.add)
+                for j in range(PACK):
+                    nc.vector.scalar_tensor_tensor(
+                        expo2[:, j, :], dots[:, j, at : at + width], row2[:, j : j + 1], cols2[:, first : first + width], ALU.add, ALU.add
+                    )
                 rounded = pool.tile([P, width, PACK], BF16, name=f"a_bf{first}", align_bytes=64)
                 nc.scalar.activation(
                     rounded[:].rearrange("p (g i) j -> p g j i", i=4),

@@ -20,7 +20,7 @@ ALU = mybir.AluOpType
 P = 128
 PACK = 4
 CHUNK = 128
-E_PLANE = 4
+SCALE_ROWS = 16
 HALF_ROW = 127
 FIRST_FILL = 64
 TINY = 2.0 ** -126
@@ -36,52 +36,60 @@ def tile_picked_ykrr_bias_p_kernel(
 
         held = ctx.enter_context(tc.tile_pool(name="held", bufs=1))
 
+        small = ctx.enter_context(tc.tile_pool(name="small", bufs=1))
         offs_t = pool.tile([P, S // 16], U16, name="offs_t")
         qry_t = pool.tile([P, V // 16], U16, name="qry_t")
         xs_win = pool.tile([P, T], U8, name="xs_win", tag="xs_bytes", align_bytes=64)
         es_win = pool.tile([P, W], U8, name="es_win", align_bytes=64)
         half_win = pool.tile([P, W], F32, name="half_win", tag="half_bytes", align_bytes=64)
 
-        zero = held.tile([P, 32], F32, name="zero", offset=480)
-        zero_rest = pool.tile([P, 1], F32, name="zero_rest", tag="ew_bytes", align_bytes=64)
+        wgt_t = pool.tile([P, PACK], F32, name="wgt_t")
+        own_t = pool.tile([P, PACK], F32, name="own_t")
+
+        zero = held.tile([P, 32], F32, name="zero", offset=4 * T - 64)
+        zero_rest = pool.tile([P, 1], F32, name="zero_rest", tag="ident_bytes", align_bytes=64)
         nc.vector.memset(xs_win[:].bitcast(I32), 0)
+        nc.vector.memset(es_win[:].bitcast(I32), 0)
         nc.vector.memset(zero[:], 0.0)
         nc.vector.memset(zero_rest[:], 0.0)
         nc.vector.tensor_copy(half_win[:HALF_ROW, :FIRST_FILL], zero[:HALF_ROW, 0:1].to_broadcast([HALF_ROW, FIRST_FILL]))
-        nc.vector.memset(es_win[:].bitcast(I32), 0)
         nc.vector.tensor_copy(half_win[:HALF_ROW, FIRST_FILL:], zero_rest[:HALF_ROW, :].to_broadcast([HALF_ROW, W - FIRST_FILL]))
-        ident = held.tile([P, P], F32, name="ident", offset=0, align_bytes=64)
-        wgt_t = held.tile([P, PACK], F32, name="wgt_t", offset=512)
-        own_t = held.tile([P, PACK], F32, name="own_t", offset=544)
-        xw_win = held.tile([P, T], U32, name="xw_win", offset=576, align_bytes=64)
-        ew_win = pool.tile([P, W], U32, name="ew_win", tag="ew_bytes", align_bytes=64)
+        xw_win = held.tile([P, T], U32, name="xw_win", offset=0, align_bytes=64)
+        ew_win = held.tile([P, W], U32, name="ew_win", offset=4 * T, align_bytes=64)
+        ident = pool.tile([P, P], F32, name="ident", tag="ident_bytes", align_bytes=64)
         make_identity(nc, ident[:])
 
-        nc.sync.dma_start(qry_t[:], qry)
-        nc.sync.dma_start(half_win[HALF_ROW : HALF_ROW + 1, :], half[0:1, :])
         nc.sync.dma_start(offs_t[:], offs)
-        for q in range(4):
-            queue = nc.sync if q % 2 == 0 else nc.scalar
-            queue.dma_start(xs_win[32 * q : 32 * q + 4, :].bitcast(I32), x_scales[0, 4 * q : 4 * q + 4, :].bitcast(I32))
-        nc.sync.dma_start(xw_win[:].bitcast(I32), x_words[0].rearrange("p n t -> p (n t)").bitcast(I32))
+        nc.sync.dma_start(qry_t[:], qry)
         nc.sync.dma_start(wgt_t[:], wgt.rearrange("(p j) o -> p (j o)", j=PACK))
-        nc.sync.dma_start(own_t[:], own.rearrange("(p j) o -> p (j o)", j=PACK))
-        for q in range(4):
-            nc.sync.dma_start(
-                es_win[32 * q + E_PLANE : 32 * q + E_PLANE + 4, :].bitcast(I32), e_scales[0, 4 * q : 4 * q + 4, :].bitcast(I32)
-            )
+        nc.scalar.dma_start(half_win[HALF_ROW : HALF_ROW + 1, :], half[0:1, :])
+        nc.scalar.dma_start(own_t[:], own.rearrange("(p j) o -> p (j o)", j=PACK))
+        nc.sync.dma_start(xs_win[:SCALE_ROWS, :].bitcast(I32), x_scales[0].bitcast(I32))
+        nc.sync.dma_start(es_win[:SCALE_ROWS, :].bitcast(I32), e_scales[0].bitcast(I32))
+        nc.sync.dma_start(xw_win[:].bitcast(I32), x_words[0].rearrange("p n t -> p (n t)").bitcast(I32))
         nc.sync.dma_start(ew_win[:].bitcast(I32), e_words[0].rearrange("p n t -> p (n t)").bitcast(I32))
 
+        mag_room = small.tile([P, 24], F32, name="mag_room", offset=0)
+        mag = mag_room[:, :PACK]
+        nc.vector.scalar_tensor_tensor(mag, wgt_t[:], -1.0, wgt_t[:], ALU.mult, ALU.max)
+
         half_picked = pool.tile([P, V], F32, name="half_picked", align_bytes=64)
-        xs_picked = pool.tile([P, S], U8, name="xs_picked", tag="picked_bytes", align_bytes=64)
-        xs_dealt = pool.tile([P, PACK, P], U8, name="xs_dealt", align_bytes=64)
-        xw_dealt = pool.tile([P, PACK, P], U32, name="xw_dealt", align_bytes=64)
         nc.vector.tensor_copy(half_picked[:], half_win[:].indirect(qry_t[:]))
+        xs_picked = pool.tile([P, S], U8, name="xs_picked", align_bytes=64)
+        es_picked = pool.tile([P, V], U8, name="es_picked", tag="xs_bytes", align_bytes=64)
+        xs_dealt = pool.tile([P, PACK, P], U8, name="xs_dealt", align_bytes=64)
+        es_placed = pool.tile([P, V], U8, name="es_placed", align_bytes=64)
         nc.vector.tensor_copy(xs_picked[:], xs_win[:].indirect(offs_t[:]))
-        nc.vector.tensor_copy(xs_dealt[:], xs_picked[:].rearrange("p (m j) -> p j m", j=PACK))
-        nc.vector.tensor_copy(xw_dealt[:].rearrange("p j m -> p m j"), xw_win[:].indirect(offs_t[:]))
-        es_picked = pool.tile([P, V], U8, name="es_picked", tag="picked_bytes", align_bytes=64)
         nc.vector.tensor_copy(es_picked[:], es_win[:].indirect(qry_t[:]))
+        nc.vector.tensor_copy(xs_dealt[:], xs_picked[:].rearrange("p (m j) -> p j m", j=PACK))
+        nc.vector.tensor_copy(es_placed[:].bitcast(I32), es_picked[:].bitcast(I32))
+        xs_rows = xs_dealt[:].rearrange("p j m -> p (j m)").bitcast(I32)
+        es_rows = es_placed[:].bitcast(I32)
+        for rows in (xs_rows, es_rows):
+            for q in range(1, 4):
+                nc.sync.dma_start(rows[32 * q : 32 * q + 4, :], rows[4 * q : 4 * q + 4, :])
+        xw_dealt = pool.tile([P, PACK, P], U32, name="xw_dealt", tag="half_bytes", align_bytes=64)
+        nc.vector.tensor_copy(xw_dealt[:].rearrange("p j m -> p m j"), xw_win[:].indirect(offs_t[:]))
 
         turned = psum.tile([P, V // P, P], F32, name="turned")
         for c in range(V // P):
@@ -91,25 +99,31 @@ def tile_picked_ykrr_bias_p_kernel(
         spread = psum.tile([P, V], F32, name="spread")
         for c in range(V // P):
             nc.tensor.transpose(spread[:, c * P : (c + 1) * P], half_col[:, c : c + 1].to_broadcast([P, P]), ident[:])
-        cols2 = pool.tile([P, V], F32, name="cols2", align_bytes=64)
-        nc.scalar.copy(cols2[:], spread[:])
 
-        mag = pool.tile([P, PACK], F32, name="mag")
-        step2 = pool.tile([P, PACK], F32, name="step2")
-        sgn = pool.tile([P, PACK], F32, name="sgn")
+        sgn = small.tile([P, PACK], F32, name="sgn", offset=32)
         log_mag = pool.tile([P, PACK], F32, name="log_mag")
-        row = pool.tile([P, PACK], F32, name="row")
+        own2 = small.tile([P, PACK], F32, name="own2", offset=64)
         row2 = pool.tile([P, PACK], F32, name="row2")
-        nc.gpsimd.tensor_scalar(step2[:], wgt_t[:], 0.0, 2.0, ALU.is_ge, ALU.mult)
-        nc.gpsimd.tensor_scalar(sgn[:], step2[:], 1.0, -1.0, ALU.mult, ALU.add)
-        nc.gpsimd.tensor_tensor(mag[:], wgt_t[:], sgn[:], ALU.mult)
-        nc.scalar.activation(log_mag[:], mag[:], ACT.Ln, bias=TINY)
-        nc.gpsimd.tensor_tensor(row[:], log_mag[:], own_t[:], ALU.add)
-        nc.gpsimd.tensor_scalar(row2[:], row[:], 2.0, 0.0, ALU.mult, ALU.add)
+        nc.scalar.activation(log_mag[:], mag, ACT.Ln, bias=TINY)
+        warm_exp = pool.tile([P, 1], F32, name="warm_exp")
+        nc.scalar.activation(warm_exp[:], log_mag[:, 0:1], ACT.Exp, scale=0.0)
+        nc.scalar.activation(own2[:], own_t[:], ACT.Copy, scale=2.0)
+        nc.scalar.activation(sgn[:], wgt_t[:], ACT.Sign, bias=TINY)
+        for j in range(PACK):
+            nc.scalar.activation(row2[:, j : j + 1], log_mag[:, j : j + 1], ACT.Identity, scale=2.0, bias=own2[:, j : j + 1])
 
-        dual_t = pool.tile([P, PACK, N], F32, name="dual_t", tag="half_bytes", align_bytes=64)
+        norms2 = []
+        for h in range(2):
+            piece = pool.tile([P, PACK, V // 2], F32, name=f"norms2_{h}", align_bytes=64)
+            for j in range(PACK):
+                nc.scalar.activation(
+                    piece[:, j, :], spread[:, h * (V // 2) : (h + 1) * (V // 2)], ACT.Identity, bias=row2[:, j : j + 1]
+                )
+            norms2.append(piece)
+
+        dual_t = pool.tile([P, PACK, N], F32, name="dual_t", tag="xs_bytes", align_bytes=64)
         nc.sync.dma_start(dual_t[:], dual.rearrange("(p j) m -> p j m", j=PACK))
-        bias_t = pool.tile([P, 1], F32, name="bias_t", tag="xs_bytes", align_bytes=64)
+        bias_t = held.tile([P, 1], F32, name="bias_t", offset=0, align_bytes=64)
         nc.sync.dma_start(bias_t[:], bias)
         dual_codes = pool.tile([P, N], U32, name="dual_codes", align_bytes=64)
         dual_scales = pool.tile([P, N], U8, name="dual_scales", align_bytes=64)
@@ -120,7 +134,7 @@ def tile_picked_ykrr_bias_p_kernel(
             nc.vector.tensor_copy(piece[:], ew_win[:].indirect(qry_t[:, h * 16 : (h + 1) * 16]))
             ew_picked.append(piece)
 
-        dual_bf = pool.tile([P, N, PACK], BF16, name="dual_bf", tag="ew_bytes", align_bytes=64)
+        dual_bf = held.tile([P, N, PACK], BF16, name="dual_bf", offset=4 * T + 64, align_bytes=64)
         nc.gpsimd.tensor_tensor(
             dual_bf[:], dual_t[:].rearrange("p j m -> p m j"), sgn[:].unsqueeze(1).to_broadcast([P, N, PACK]), ALU.mult
         )
@@ -135,7 +149,7 @@ def tile_picked_ykrr_bias_p_kernel(
                     lhsT=xw_dealt[:, j, :].bitcast(FP8X4),
                     lhsT_scale=xs_dealt[:, j, :],
                     rhs=ew_picked[h][:, lo : lo + CHUNK].bitcast(FP8X4),
-                    rhs_scale=es_picked[E_PLANE:P, c * CHUNK : (c + 1) * CHUNK],
+                    rhs_scale=es_placed[:, c * CHUNK : (c + 1) * CHUNK],
                     start=True,
                     stop=True,
                 )
@@ -143,10 +157,7 @@ def tile_picked_ykrr_bias_p_kernel(
             for at in range(0, CHUNK, width):
                 first = c * CHUNK + at
                 expo2 = pool.tile([P, PACK, width], F32, name=f"expo2_{first}", align_bytes=64)
-                for j in range(PACK):
-                    nc.vector.scalar_tensor_tensor(
-                        expo2[:, j, :], dots[:, j, at : at + width], row2[:, j : j + 1], cols2[:, first : first + width], ALU.add, ALU.add
-                    )
+                nc.vector.tensor_tensor(expo2[:], dots[:, :, at : at + width], norms2[h][:, :, lo + at : lo + at + width], ALU.add)
                 rounded = pool.tile([P, width, PACK], BF16, name=f"a_bf{first}", align_bytes=64)
                 nc.scalar.activation(
                     rounded[:].rearrange("p (g i) j -> p g j i", i=4),

@@ -21,6 +21,7 @@ P = 128
 PACK = 4
 CHUNK = 128
 SCALE_ROWS = 16
+X_ROW = P - SCALE_ROWS
 HALF_ROW = 127
 FIRST_FILL = 64
 TINY = 2.0 ** -126
@@ -40,65 +41,67 @@ def tile_picked_ykrr_bias_p_kernel(
         offs_t = pool.tile([P, S // 16], U16, name="offs_t")
         qry_t = pool.tile([P, V // 16], U16, name="qry_t")
         xs_win = pool.tile([P, T], U8, name="xs_win", tag="xs_bytes", align_bytes=64)
-        es_win = pool.tile([P, W], U8, name="es_win", align_bytes=64)
+        es_win = pool.tile([P, W], U8, name="es_win", tag="es_bytes", align_bytes=64)
         half_win = pool.tile([P, W], F32, name="half_win", tag="half_bytes", align_bytes=64)
 
         wgt_t = pool.tile([P, PACK], F32, name="wgt_t")
         own_t = pool.tile([P, PACK], F32, name="own_t")
 
-        zero = held.tile([P, 32], F32, name="zero", offset=4 * T - 64)
-        zero_rest = pool.tile([P, 1], F32, name="zero_rest", tag="ident_bytes", align_bytes=64)
-        nc.vector.memset(xs_win[:].bitcast(I32), 0)
-        nc.vector.memset(es_win[:].bitcast(I32), 0)
+        zero = pool.tile([P, 1], F32, name="zero", tag="xw_bytes", align_bytes=64)
+        zero_rest = held.tile([P, 32], F32, name="zero_rest", offset=4 * P - 64)
         nc.vector.memset(zero[:], 0.0)
         nc.vector.memset(zero_rest[:], 0.0)
         nc.vector.tensor_copy(half_win[:HALF_ROW, :FIRST_FILL], zero[:HALF_ROW, 0:1].to_broadcast([HALF_ROW, FIRST_FILL]))
-        nc.vector.tensor_copy(half_win[:HALF_ROW, FIRST_FILL:], zero_rest[:HALF_ROW, :].to_broadcast([HALF_ROW, W - FIRST_FILL]))
-        xw_win = held.tile([P, T], U32, name="xw_win", offset=0, align_bytes=64)
-        ew_win = held.tile([P, W], U32, name="ew_win", offset=4 * T, align_bytes=64)
-        ident = pool.tile([P, P], F32, name="ident", tag="ident_bytes", align_bytes=64)
+        nc.vector.memset(es_win[:].bitcast(I32), 0)
+        nc.vector.memset(xs_win[:X_ROW, :].bitcast(I32), 0)
+        nc.vector.tensor_copy(half_win[:HALF_ROW, FIRST_FILL:], zero_rest[:HALF_ROW, 0:1].to_broadcast([HALF_ROW, W - FIRST_FILL]))
+        xw_win = pool.tile([P, T], U32, name="xw_win", tag="xw_bytes", align_bytes=64)
+        ident = held.tile([P, P], F32, name="ident", offset=0, align_bytes=64)
+        ew_win = held.tile([P, W], U32, name="ew_win", offset=4 * P, align_bytes=64)
         make_identity(nc, ident[:])
 
         nc.sync.dma_start(offs_t[:], offs)
+        nc.sync.dma_start(xs_win[X_ROW:, :].bitcast(I32), x_scales[0].bitcast(I32))
         nc.sync.dma_start(qry_t[:], qry)
-        nc.sync.dma_start(wgt_t[:], wgt.rearrange("(p j) o -> p (j o)", j=PACK))
+        nc.scalar.dma_start(wgt_t[:], wgt.rearrange("(p j) o -> p (j o)", j=PACK))
         nc.scalar.dma_start(half_win[HALF_ROW : HALF_ROW + 1, :], half[0:1, :])
         nc.scalar.dma_start(own_t[:], own.rearrange("(p j) o -> p (j o)", j=PACK))
-        nc.sync.dma_start(xs_win[:SCALE_ROWS, :].bitcast(I32), x_scales[0].bitcast(I32))
-        nc.sync.dma_start(es_win[:SCALE_ROWS, :].bitcast(I32), e_scales[0].bitcast(I32))
         nc.sync.dma_start(xw_win[:].bitcast(I32), x_words[0].rearrange("p n t -> p (n t)").bitcast(I32))
+        for q in range(4):
+            nc.sync.dma_start(es_win[32 * q : 32 * q + 4, :].bitcast(I32), e_scales[0, 4 * q : 4 * q + 4, :].bitcast(I32))
         nc.sync.dma_start(ew_win[:].bitcast(I32), e_words[0].rearrange("p n t -> p (n t)").bitcast(I32))
 
         mag_room = small.tile([P, 24], F32, name="mag_room", offset=0)
         mag = mag_room[:, :PACK]
         nc.vector.scalar_tensor_tensor(mag, wgt_t[:], -1.0, wgt_t[:], ALU.mult, ALU.max)
 
-        half_picked = pool.tile([P, V], F32, name="half_picked", align_bytes=64)
-        nc.vector.tensor_copy(half_picked[:], half_win[:].indirect(qry_t[:]))
-        xs_picked = pool.tile([P, S], U8, name="xs_picked", align_bytes=64)
-        es_picked = pool.tile([P, V], U8, name="es_picked", tag="xs_bytes", align_bytes=64)
+        xs_picked = pool.tile([P, S], U8, name="xs_picked", tag="picked_bytes", align_bytes=64)
         xs_dealt = pool.tile([P, PACK, P], U8, name="xs_dealt", align_bytes=64)
-        es_placed = pool.tile([P, V], U8, name="es_placed", align_bytes=64)
+        half_picked = pool.tile([P, V], F32, name="half_picked", align_bytes=64)
+        xw_dealt = pool.tile([P, PACK, P], U32, name="xw_dealt", align_bytes=64)
         nc.vector.tensor_copy(xs_picked[:], xs_win[:].indirect(offs_t[:]))
-        nc.vector.tensor_copy(es_picked[:], es_win[:].indirect(qry_t[:]))
+        nc.vector.tensor_copy(half_picked[:], half_win[:].indirect(qry_t[:]))
         nc.vector.tensor_copy(xs_dealt[:], xs_picked[:].rearrange("p (m j) -> p j m", j=PACK))
-        nc.vector.tensor_copy(es_placed[:].bitcast(I32), es_picked[:].bitcast(I32))
         xs_rows = xs_dealt[:].rearrange("p j m -> p (j m)").bitcast(I32)
-        es_rows = es_placed[:].bitcast(I32)
-        for rows in (xs_rows, es_rows):
-            for q in range(1, 4):
-                nc.sync.dma_start(rows[32 * q : 32 * q + 4, :], rows[4 * q : 4 * q + 4, :])
-        xw_dealt = pool.tile([P, PACK, P], U32, name="xw_dealt", tag="half_bytes", align_bytes=64)
+        for q in range(4):
+            nc.sync.dma_start(xs_rows[32 * q : 32 * q + 4, :], xs_rows[X_ROW + 4 * q : X_ROW + 4 * q + 4, :])
+        dual_t = pool.tile([P, PACK, N], F32, name="dual_t", tag="half_bytes", align_bytes=64)
+        nc.sync.dma_start(dual_t[:], dual.rearrange("(p j) m -> p j m", j=PACK))
         nc.vector.tensor_copy(xw_dealt[:].rearrange("p j m -> p m j"), xw_win[:].indirect(offs_t[:]))
+        es_picked = pool.tile([P, V], U8, name="es_picked", tag="picked_bytes", align_bytes=64)
+        nc.vector.tensor_copy(es_picked[:], es_win[:].indirect(qry_t[:]))
 
-        turned = psum.tile([P, V // P, P], F32, name="turned")
-        for c in range(V // P):
-            nc.tensor.transpose(turned[:, c, :], half_picked[:, c * P : (c + 1) * P], ident[:])
-        half_col = pool.tile([P, V // P], F32, name="half_col")
-        nc.scalar.activation(half_col[:], turned[:, :, HALF_ROW], ACT.Copy, scale=-2.0)
-        spread = psum.tile([P, V], F32, name="spread")
-        for c in range(V // P):
-            nc.tensor.transpose(spread[:, c * P : (c + 1) * P], half_col[:, c : c + 1].to_broadcast([P, P]), ident[:])
+        spread = []
+        for h in range(2):
+            turned = psum.tile([P, 2, P], F32, name=f"turned{h}")
+            for c in range(2):
+                nc.tensor.transpose(turned[:, c, :], half_picked[:, (2 * h + c) * P : (2 * h + c + 1) * P], ident[:])
+            half_col = pool.tile([P, 2], F32, name=f"half_col{h}")
+            nc.scalar.activation(half_col[:], turned[:, :, HALF_ROW], ACT.Copy, scale=-2.0)
+            wide = psum.tile([P, V // 2], F32, name=f"spread{h}")
+            for c in range(2):
+                nc.tensor.transpose(wide[:, c * P : (c + 1) * P], half_col[:, c : c + 1].to_broadcast([P, P]), ident[:])
+            spread.append(wide)
 
         sgn = small.tile([P, PACK], F32, name="sgn", offset=32)
         log_mag = pool.tile([P, PACK], F32, name="log_mag")
@@ -116,16 +119,11 @@ def tile_picked_ykrr_bias_p_kernel(
         for h in range(2):
             piece = pool.tile([P, PACK, V // 2], F32, name=f"norms2_{h}", align_bytes=64)
             for j in range(PACK):
-                nc.scalar.activation(
-                    piece[:, j, :], spread[:, h * (V // 2) : (h + 1) * (V // 2)], ACT.Identity, bias=row2[:, j : j + 1]
-                )
+                nc.scalar.activation(piece[:, j, :], spread[h][:], ACT.Identity, bias=row2[:, j : j + 1])
             norms2.append(piece)
 
-        dual_t = pool.tile([P, PACK, N], F32, name="dual_t", tag="xs_bytes", align_bytes=64)
-        nc.sync.dma_start(dual_t[:], dual.rearrange("(p j) m -> p j m", j=PACK))
-        bias_t = held.tile([P, 1], F32, name="bias_t", offset=0, align_bytes=64)
+        bias_t = pool.tile([P, 1], F32, name="bias_t", tag="xw_bytes", align_bytes=64)
         nc.sync.dma_start(bias_t[:], bias)
-        dual_codes = pool.tile([P, N], U32, name="dual_codes", align_bytes=64)
         dual_scales = pool.tile([P, N], U8, name="dual_scales", align_bytes=64)
 
         ew_picked = []
@@ -134,7 +132,7 @@ def tile_picked_ykrr_bias_p_kernel(
             nc.vector.tensor_copy(piece[:], ew_win[:].indirect(qry_t[:, h * 16 : (h + 1) * 16]))
             ew_picked.append(piece)
 
-        dual_bf = held.tile([P, N, PACK], BF16, name="dual_bf", offset=4 * T + 64, align_bytes=64)
+        dual_bf = pool.tile([P, N, PACK], BF16, name="dual_bf", align_bytes=64)
         nc.gpsimd.tensor_tensor(
             dual_bf[:], dual_t[:].rearrange("p j m -> p m j"), sgn[:].unsqueeze(1).to_broadcast([P, N, PACK]), ALU.mult
         )
@@ -149,14 +147,14 @@ def tile_picked_ykrr_bias_p_kernel(
                     lhsT=xw_dealt[:, j, :].bitcast(FP8X4),
                     lhsT_scale=xs_dealt[:, j, :],
                     rhs=ew_picked[h][:, lo : lo + CHUNK].bitcast(FP8X4),
-                    rhs_scale=es_placed[:, c * CHUNK : (c + 1) * CHUNK],
+                    rhs_scale=es_picked[:, c * CHUNK : (c + 1) * CHUNK],
                     start=True,
                     stop=True,
                 )
             width = CHUNK if c < V // CHUNK - 1 else CHUNK // 2
             for at in range(0, CHUNK, width):
                 first = c * CHUNK + at
-                expo2 = pool.tile([P, PACK, width], F32, name=f"expo2_{first}", align_bytes=64)
+                expo2 = pool.tile([P, PACK, width], F32, name=f"expo2_{first}", tag=f"expo_bytes{first}", align_bytes=64)
                 nc.vector.tensor_tensor(expo2[:], dots[:, :, at : at + width], norms2[h][:, :, lo + at : lo + at + width], ALU.add)
                 rounded = pool.tile([P, width, PACK], BF16, name=f"a_bf{first}", align_bytes=64)
                 nc.scalar.activation(
@@ -167,12 +165,13 @@ def tile_picked_ykrr_bias_p_kernel(
                 )
                 spans.append((first, width, rounded))
 
+        dual_codes = pool.tile([P, N], U32, name="dual_codes", tag="expo_bytes0", align_bytes=64)
         nc.vector.quantize_mx(out=dual_codes[:].bitcast(FP8X4), scales=dual_scales[:], in_=dual_bf[:].rearrange("p m j -> p (m j)"))
         for n, (first, width, rounded) in enumerate(spans):
             a_codes = pool.tile([P, width], U32, name=f"a_codes{first}", align_bytes=64)
             a_scales = pool.tile([P, width], U8, name=f"a_scales{first}", align_bytes=64)
             nc.vector.quantize_mx(out=a_codes[:].bitcast(FP8X4), scales=a_scales[:], in_=rounded[:].rearrange("p v j -> p (v j)"))
-            acc = psum.tile([P, width], F32, name=f"acc{n}", tag=["acc0", "acc1", "turned", "spread", "dots0"][n])
+            acc = psum.tile([P, width], F32, name=f"acc{n}", tag=["turned0", "turned1", "spread0", "spread1", "dots0"][n])
             nc.tensor.matmul_mx(
                 out=acc[:],
                 lhsT=dual_codes[:].bitcast(FP8X4),

@@ -24,6 +24,7 @@ SCALE_ROWS = 16
 X_ROW = P - SCALE_ROWS
 HALF_ROW = 127
 FIRST_FILL = 64
+VECTOR_FILL = 1408
 TINY = 2.0 ** -126
 
 
@@ -54,26 +55,31 @@ def tile_picked_ykrr_bias_p_kernel(
         nc.vector.tensor_copy(half_win[:HALF_ROW, :FIRST_FILL], zero[:HALF_ROW, 0:1].to_broadcast([HALF_ROW, FIRST_FILL]))
         nc.vector.memset(es_win[:].bitcast(I32), 0)
         nc.vector.memset(xs_win[:X_ROW, :].bitcast(I32), 0)
-        nc.vector.tensor_copy(half_win[:HALF_ROW, FIRST_FILL:], zero_rest[:HALF_ROW, 0:1].to_broadcast([HALF_ROW, W - FIRST_FILL]))
+        nc.vector.tensor_copy(
+            half_win[:HALF_ROW, FIRST_FILL:VECTOR_FILL], zero_rest[:HALF_ROW, 0:1].to_broadcast([HALF_ROW, VECTOR_FILL - FIRST_FILL])
+        )
         xw_win = pool.tile([P, T], U32, name="xw_win", tag="xw_bytes", align_bytes=64)
         ident = held.tile([P, P], F32, name="ident", offset=0, align_bytes=64)
         ew_win = held.tile([P, W], U32, name="ew_win", offset=4 * P, align_bytes=64)
         make_identity(nc, ident[:])
 
         nc.sync.dma_start(offs_t[:], offs)
-        nc.sync.dma_start(xs_win[X_ROW:, :].bitcast(I32), x_scales[0].bitcast(I32))
+        nc.scalar.dma_start(xs_win[X_ROW:, :].bitcast(I32), x_scales[0].bitcast(I32))
         nc.sync.dma_start(qry_t[:], qry)
-        nc.scalar.dma_start(wgt_t[:], wgt.rearrange("(p j) o -> p (j o)", j=PACK))
         nc.scalar.dma_start(half_win[HALF_ROW : HALF_ROW + 1, :], half[0:1, :])
-        nc.scalar.dma_start(own_t[:], own.rearrange("(p j) o -> p (j o)", j=PACK))
+        nc.sync.dma_start(wgt_t[:], wgt.rearrange("(p j) o -> p (j o)", j=PACK))
+        nc.sync.dma_start(own_t[:], own.rearrange("(p j) o -> p (j o)", j=PACK))
         nc.sync.dma_start(xw_win[:].bitcast(I32), x_words[0].rearrange("p n t -> p (n t)").bitcast(I32))
         for q in range(4):
             nc.sync.dma_start(es_win[32 * q : 32 * q + 4, :].bitcast(I32), e_scales[0, 4 * q : 4 * q + 4, :].bitcast(I32))
         nc.sync.dma_start(ew_win[:].bitcast(I32), e_words[0].rearrange("p n t -> p (n t)").bitcast(I32))
 
+        nc.scalar.activation(
+            half_win[:HALF_ROW, VECTOR_FILL:], half_win[:HALF_ROW, 0:1].to_broadcast([HALF_ROW, W - VECTOR_FILL]), ACT.Ln, bias=1.0
+        )
         mag_room = small.tile([P, 24], F32, name="mag_room", offset=0)
         mag = mag_room[:, :PACK]
-        nc.vector.scalar_tensor_tensor(mag, wgt_t[:], -1.0, wgt_t[:], ALU.mult, ALU.max)
+        nc.scalar.activation(mag, wgt_t[:], ACT.Abs)
 
         xs_picked = pool.tile([P, S], U8, name="xs_picked", tag="picked_bytes", align_bytes=64)
         xs_dealt = pool.tile([P, PACK, P], U8, name="xs_dealt", align_bytes=64)
@@ -92,15 +98,15 @@ def tile_picked_ykrr_bias_p_kernel(
         nc.vector.tensor_copy(es_picked[:], es_win[:].indirect(qry_t[:]))
 
         spread = []
-        for h in range(2):
-            turned = psum.tile([P, 2, P], F32, name=f"turned{h}")
-            for c in range(2):
-                nc.tensor.transpose(turned[:, c, :], half_picked[:, (2 * h + c) * P : (2 * h + c + 1) * P], ident[:])
-            half_col = pool.tile([P, 2], F32, name=f"half_col{h}")
+        for h, chunks in enumerate(([0], [1, 2, 3])):
+            turned = psum.tile([P, len(chunks), P], F32, name=f"turned{h}")
+            for n, c in enumerate(chunks):
+                nc.tensor.transpose(turned[:, n, :], half_picked[:, c * P : (c + 1) * P], ident[:])
+            half_col = pool.tile([P, len(chunks)], F32, name=f"half_col{h}")
             nc.scalar.activation(half_col[:], turned[:, :, HALF_ROW], ACT.Copy, scale=-2.0)
-            wide = psum.tile([P, V // 2], F32, name=f"spread{h}")
-            for c in range(2):
-                nc.tensor.transpose(wide[:, c * P : (c + 1) * P], half_col[:, c : c + 1].to_broadcast([P, P]), ident[:])
+            wide = psum.tile([P, len(chunks) * P], F32, name=f"spread{h}")
+            for n in range(len(chunks)):
+                nc.tensor.transpose(wide[:, n * P : (n + 1) * P], half_col[:, n : n + 1].to_broadcast([P, P]), ident[:])
             spread.append(wide)
 
         sgn = small.tile([P, PACK], F32, name="sgn", offset=32)
@@ -117,7 +123,7 @@ def tile_picked_ykrr_bias_p_kernel(
 
         norms2 = []
         for h in range(2):
-            piece = pool.tile([P, PACK, V // 2], F32, name=f"norms2_{h}", align_bytes=64)
+            piece = pool.tile([P, PACK, CHUNK if h == 0 else V - CHUNK], F32, name=f"norms2_{h}", align_bytes=64)
             for j in range(PACK):
                 nc.scalar.activation(piece[:, j, :], spread[h][:], ACT.Identity, bias=row2[:, j : j + 1])
             norms2.append(piece)
@@ -132,7 +138,7 @@ def tile_picked_ykrr_bias_p_kernel(
             nc.vector.tensor_copy(piece[:], ew_win[:].indirect(qry_t[:, h * 16 : (h + 1) * 16]))
             ew_picked.append(piece)
 
-        dual_bf = pool.tile([P, N, PACK], BF16, name="dual_bf", align_bytes=64)
+        dual_bf = held.tile([P, N, PACK], BF16, name="dual_bf", offset=4 * P, align_bytes=64)
         nc.gpsimd.tensor_tensor(
             dual_bf[:], dual_t[:].rearrange("p j m -> p m j"), sgn[:].unsqueeze(1).to_broadcast([P, N, PACK]), ALU.mult
         )
@@ -151,19 +157,25 @@ def tile_picked_ykrr_bias_p_kernel(
                     start=True,
                     stop=True,
                 )
-            width = CHUNK if c < V // CHUNK - 1 else CHUNK // 2
+            width = CHUNK if 0 < c < V // CHUNK - 1 else CHUNK // 2
             for at in range(0, CHUNK, width):
                 first = c * CHUNK + at
+                terms = first if c == 0 else first - CHUNK
                 expo2 = pool.tile([P, PACK, width], F32, name=f"expo2_{first}", tag=f"expo_bytes{first}", align_bytes=64)
-                nc.vector.tensor_tensor(expo2[:], dots[:, :, at : at + width], norms2[h][:, :, lo + at : lo + at + width], ALU.add)
-                rounded = pool.tile([P, width, PACK], BF16, name=f"a_bf{first}", align_bytes=64)
+                nc.vector.tensor_tensor(expo2[:], dots[:, :, at : at + width], norms2[min(c, 1)][:, :, terms : terms + width], ALU.add)
+                if c > 0 or at == 0:
+                    rounded = pool.tile([P, CHUNK if c == 0 else width, PACK], BF16, name=f"a_bf{first}", align_bytes=64)
+                into = rounded[:, at : at + width, :] if c == 0 else rounded[:]
                 nc.scalar.activation(
-                    rounded[:].rearrange("p (g i) j -> p g j i", i=4),
+                    into.rearrange("p (g i) j -> p g j i", i=4),
                     expo2[:].rearrange("p j (g i) -> p g j i", i=4),
                     ACT.Exp,
                     scale=0.5,
                 )
-                spans.append((first, width, rounded))
+                if c > 0:
+                    spans.append((first, width, rounded))
+                elif at > 0:
+                    spans.append((0, CHUNK, rounded))
 
         dual_codes = pool.tile([P, N], U32, name="dual_codes", tag="expo_bytes0", align_bytes=64)
         nc.vector.quantize_mx(out=dual_codes[:].bitcast(FP8X4), scales=dual_scales[:], in_=dual_bf[:].rearrange("p m j -> p (m j)"))

@@ -39,6 +39,7 @@ def tile_picked_ykrr_bias_p_kernel(
         held = ctx.enter_context(tc.tile_pool(name="held", bufs=1))
 
         small = ctx.enter_context(tc.tile_pool(name="small", bufs=1))
+        after_xw = ctx.enter_context(tc.tile_pool(name="after_xw", bufs=1))
         offs_t = pool.tile([P, S // 16], U16, name="offs_t")
         qry_t = pool.tile([P, V // 16], U16, name="qry_t")
         xs_win = pool.tile([P, T], U8, name="xs_win", tag="xs_bytes", align_bytes=64)
@@ -48,7 +49,7 @@ def tile_picked_ykrr_bias_p_kernel(
         wgt_t = pool.tile([P, PACK], F32, name="wgt_t")
         own_t = pool.tile([P, PACK], F32, name="own_t")
 
-        zero = pool.tile([P, 1], F32, name="zero", tag="xw_bytes", align_bytes=64)
+        zero = after_xw.tile([P, 1], F32, name="zero", offset=0)
         zero_rest = held.tile([P, 32], F32, name="zero_rest", offset=4 * P - 64)
         nc.vector.memset(zero[:], 0.0)
         nc.vector.memset(zero_rest[:], 0.0)
@@ -58,7 +59,7 @@ def tile_picked_ykrr_bias_p_kernel(
         nc.vector.tensor_copy(
             half_win[:HALF_ROW, FIRST_FILL:VECTOR_FILL], zero_rest[:HALF_ROW, 0:1].to_broadcast([HALF_ROW, VECTOR_FILL - FIRST_FILL])
         )
-        xw_win = pool.tile([P, T], U32, name="xw_win", tag="xw_bytes", align_bytes=64)
+        xw_win = after_xw.tile([P, T], U32, name="xw_win", offset=0, align_bytes=64)
         ident = held.tile([P, P], F32, name="ident", offset=0, align_bytes=64)
         ew_win = held.tile([P, W], U32, name="ew_win", offset=4 * P, align_bytes=64)
         make_identity(nc, ident[:])
@@ -91,8 +92,6 @@ def tile_picked_ykrr_bias_p_kernel(
         xs_rows = xs_dealt[:].rearrange("p j m -> p (j m)").bitcast(I32)
         for q in range(4):
             nc.sync.dma_start(xs_rows[32 * q : 32 * q + 4, :], xs_rows[X_ROW + 4 * q : X_ROW + 4 * q + 4, :])
-        dual_t = pool.tile([P, PACK, N], F32, name="dual_t", tag="half_bytes", align_bytes=64)
-        nc.sync.dma_start(dual_t[:], dual.rearrange("(p j) m -> p j m", j=PACK))
         nc.vector.tensor_copy(xw_dealt[:].rearrange("p j m -> p m j"), xw_win[:].indirect(offs_t[:]))
         es_picked = pool.tile([P, V], U8, name="es_picked", tag="picked_bytes", align_bytes=64)
         nc.vector.tensor_copy(es_picked[:], es_win[:].indirect(qry_t[:]))
@@ -128,7 +127,9 @@ def tile_picked_ykrr_bias_p_kernel(
                 nc.scalar.activation(piece[:, j, :], spread[h][:], ACT.Identity, bias=row2[:, j : j + 1])
             norms2.append(piece)
 
-        bias_t = pool.tile([P, 1], F32, name="bias_t", tag="xw_bytes", align_bytes=64)
+        dual_t = after_xw.tile([P, PACK, N], F32, name="dual_t", offset=0, align_bytes=64)
+        nc.sync.dma_start(dual_t[:], dual.rearrange("(p j) m -> p j m", j=PACK))
+        bias_t = after_xw.tile([P, 1], F32, name="bias_t", offset=4 * PACK * N, align_bytes=64)
         nc.sync.dma_start(bias_t[:], bias)
         dual_scales = pool.tile([P, N], U8, name="dual_scales", align_bytes=64)
 

@@ -24,8 +24,8 @@ SCALE_ROWS = 16
 X_ROW = P - SCALE_ROWS
 HALF_ROW = 127
 FIRST_FILL = 64
-VECTOR_FILL = 1408
-TINY = 2.0 ** -126
+VECTOR_FILL = 1920
+TINY = 2.0 ** -64
 
 
 def tile_picked_ykrr_bias_p_kernel(
@@ -38,7 +38,6 @@ def tile_picked_ykrr_bias_p_kernel(
 
         held = ctx.enter_context(tc.tile_pool(name="held", bufs=1))
 
-        small = ctx.enter_context(tc.tile_pool(name="small", bufs=1))
         after_xw = ctx.enter_context(tc.tile_pool(name="after_xw", bufs=1))
         offs_t = pool.tile([P, S // 16], U16, name="offs_t")
         qry_t = pool.tile([P, V // 16], U16, name="qry_t")
@@ -49,15 +48,14 @@ def tile_picked_ykrr_bias_p_kernel(
         wgt_t = pool.tile([P, PACK], F32, name="wgt_t")
         own_t = pool.tile([P, PACK], F32, name="own_t")
 
-        zero = after_xw.tile([P, 1], F32, name="zero", offset=0)
-        zero_rest = held.tile([P, 32], F32, name="zero_rest", offset=4 * P - 64)
+        zero = held.tile([P, 16], F32, name="zero", offset=4 * P - 32)
         nc.vector.memset(zero[:], 0.0)
-        nc.vector.memset(zero_rest[:], 0.0)
+        nc.vector.memset(xs_win[:X_ROW, :].bitcast(I32), 0)
         nc.vector.tensor_copy(half_win[:HALF_ROW, :FIRST_FILL], zero[:HALF_ROW, 0:1].to_broadcast([HALF_ROW, FIRST_FILL]))
         nc.vector.memset(es_win[:].bitcast(I32), 0)
-        nc.vector.memset(xs_win[:X_ROW, :].bitcast(I32), 0)
         nc.vector.tensor_copy(
-            half_win[:HALF_ROW, FIRST_FILL:VECTOR_FILL], zero_rest[:HALF_ROW, 0:1].to_broadcast([HALF_ROW, VECTOR_FILL - FIRST_FILL])
+            half_win[:HALF_ROW, FIRST_FILL:VECTOR_FILL].rearrange("p (g i) -> p g i", i=16),
+            zero[:HALF_ROW, :].unsqueeze(1).to_broadcast([HALF_ROW, (VECTOR_FILL - FIRST_FILL) // 16, 16]),
         )
         xw_win = after_xw.tile([P, T], U32, name="xw_win", offset=0, align_bytes=64)
         ident = held.tile([P, P], F32, name="ident", offset=0, align_bytes=64)
@@ -72,15 +70,25 @@ def tile_picked_ykrr_bias_p_kernel(
         nc.sync.dma_start(own_t[:], own.rearrange("(p j) o -> p (j o)", j=PACK))
         nc.sync.dma_start(xw_win[:].bitcast(I32), x_words[0].rearrange("p n t -> p (n t)").bitcast(I32))
         for q in range(4):
-            nc.sync.dma_start(es_win[32 * q : 32 * q + 4, :].bitcast(I32), e_scales[0, 4 * q : 4 * q + 4, :].bitcast(I32))
+            nc.sync.dma_start(es_win[q::32, :].bitcast(I32), e_scales[0, q::4, :].bitcast(I32))
         nc.sync.dma_start(ew_win[:].bitcast(I32), e_words[0].rearrange("p n t -> p (n t)").bitcast(I32))
 
         nc.scalar.activation(
             half_win[:HALF_ROW, VECTOR_FILL:], half_win[:HALF_ROW, 0:1].to_broadcast([HALF_ROW, W - VECTOR_FILL]), ACT.Ln, bias=1.0
         )
-        mag_room = small.tile([P, 24], F32, name="mag_room", offset=0)
-        mag = mag_room[:, :PACK]
-        nc.scalar.activation(mag, wgt_t[:], ACT.Abs)
+        mag = pool.tile([P, PACK], F32, name="mag")
+        sgn = pool.tile([P, PACK], F32, name="sgn")
+        own2 = pool.tile([P, PACK], F32, name="own2")
+        log_mag = pool.tile([P, PACK], F32, name="log_mag")
+        row2 = pool.tile([P, PACK], F32, name="row2")
+        nc.scalar.activation(mag[:], wgt_t[:], ACT.Abs)
+        nc.scalar.activation(sgn[:], wgt_t[:], ACT.Sign, bias=TINY)
+        nc.scalar.activation(own2[:], own_t[:], ACT.Copy, scale=2.0)
+        nc.scalar.activation(log_mag[:], mag[:], ACT.Ln, bias=TINY)
+        warm_exp = pool.tile([P, 1], F32, name="warm_exp")
+        nc.scalar.activation(warm_exp[:], log_mag[:, 0:1], ACT.Exp, scale=0.0)
+        for j in range(PACK):
+            nc.scalar.activation(row2[:, j : j + 1], log_mag[:, j : j + 1], ACT.Identity, scale=2.0, bias=own2[:, j : j + 1])
 
         xs_picked = pool.tile([P, S], U8, name="xs_picked", tag="picked_bytes", align_bytes=64)
         xs_dealt = pool.tile([P, PACK, P], U8, name="xs_dealt", align_bytes=64)
@@ -107,18 +115,6 @@ def tile_picked_ykrr_bias_p_kernel(
             for n in range(len(chunks)):
                 nc.tensor.transpose(wide[:, n * P : (n + 1) * P], half_col[:, n : n + 1].to_broadcast([P, P]), ident[:])
             spread.append(wide)
-
-        sgn = small.tile([P, PACK], F32, name="sgn", offset=32)
-        log_mag = pool.tile([P, PACK], F32, name="log_mag")
-        own2 = small.tile([P, PACK], F32, name="own2", offset=64)
-        row2 = pool.tile([P, PACK], F32, name="row2")
-        nc.scalar.activation(log_mag[:], mag, ACT.Ln, bias=TINY)
-        warm_exp = pool.tile([P, 1], F32, name="warm_exp")
-        nc.scalar.activation(warm_exp[:], log_mag[:, 0:1], ACT.Exp, scale=0.0)
-        nc.scalar.activation(own2[:], own_t[:], ACT.Copy, scale=2.0)
-        nc.scalar.activation(sgn[:], wgt_t[:], ACT.Sign, bias=TINY)
-        for j in range(PACK):
-            nc.scalar.activation(row2[:, j : j + 1], log_mag[:, j : j + 1], ACT.Identity, scale=2.0, bias=own2[:, j : j + 1])
 
         norms2 = []
         for h in range(2):

@@ -24,7 +24,6 @@ SCALE_ROWS = 16
 X_ROW = P - SCALE_ROWS
 HALF_ROW = 127
 FIRST_FILL = 64
-VECTOR_FILL = 1920
 TINY = 2.0 ** -64
 
 
@@ -46,7 +45,7 @@ def tile_picked_ykrr_bias_p_kernel(
         half_win = pool.tile([P, W], F32, name="half_win", tag="half_bytes", align_bytes=64)
 
         wgt_t = pool.tile([P, PACK], F32, name="wgt_t")
-        own_t = pool.tile([P, PACK], F32, name="own_t")
+        own_row = pool.tile([P, S], F32, name="own_row", align_bytes=64)
 
         zero = held.tile([P, 16], F32, name="zero", offset=4 * P - 32)
         nc.vector.memset(zero[:], 0.0)
@@ -54,8 +53,8 @@ def tile_picked_ykrr_bias_p_kernel(
         nc.vector.tensor_copy(half_win[:HALF_ROW, :FIRST_FILL], zero[:HALF_ROW, 0:1].to_broadcast([HALF_ROW, FIRST_FILL]))
         nc.vector.memset(es_win[:].bitcast(I32), 0)
         nc.vector.tensor_copy(
-            half_win[:HALF_ROW, FIRST_FILL:VECTOR_FILL].rearrange("p (g i) -> p g i", i=16),
-            zero[:HALF_ROW, :].unsqueeze(1).to_broadcast([HALF_ROW, (VECTOR_FILL - FIRST_FILL) // 16, 16]),
+            half_win[:HALF_ROW, FIRST_FILL:W].rearrange("p (g i) -> p g i", i=16),
+            zero[:HALF_ROW, :].unsqueeze(1).to_broadcast([HALF_ROW, (W - FIRST_FILL) // 16, 16]),
         )
         xw_win = after_xw.tile([P, T], U32, name="xw_win", offset=0, align_bytes=64)
         ident = held.tile([P, P], F32, name="ident", offset=0, align_bytes=64)
@@ -67,14 +66,14 @@ def tile_picked_ykrr_bias_p_kernel(
         nc.sync.dma_start(qry_t[:], qry)
         nc.scalar.dma_start(half_win[HALF_ROW : HALF_ROW + 1, :], half[0:1, :])
         nc.sync.dma_start(wgt_t[:], wgt.rearrange("(p j) o -> p (j o)", j=PACK))
-        nc.sync.dma_start(own_t[:], own.rearrange("(p j) o -> p (j o)", j=PACK))
+        nc.sync.dma_start(own_row[HALF_ROW:, :], own.rearrange("t o -> o t"))
         nc.sync.dma_start(xw_win[:].bitcast(I32), x_words[0].rearrange("p n t -> p (n t)").bitcast(I32))
         for q in range(4):
             nc.sync.dma_start(es_win[q::32, :].bitcast(I32), e_scales[0, q::4, :].bitcast(I32))
         nc.sync.dma_start(ew_win[:].bitcast(I32), e_words[0].rearrange("p n t -> p (n t)").bitcast(I32))
 
         nc.scalar.activation(
-            half_win[:HALF_ROW, VECTOR_FILL:], half_win[:HALF_ROW, 0:1].to_broadcast([HALF_ROW, W - VECTOR_FILL]), ACT.Ln, bias=1.0
+            own_row[:HALF_ROW, :], half_win[:HALF_ROW, 0:1].to_broadcast([HALF_ROW, S]), ACT.Ln, bias=1.0
         )
         mag = pool.tile([P, PACK], F32, name="mag")
         sgn = pool.tile([P, PACK], F32, name="sgn")
@@ -83,10 +82,13 @@ def tile_picked_ykrr_bias_p_kernel(
         row2 = pool.tile([P, PACK], F32, name="row2")
         nc.scalar.activation(mag[:], wgt_t[:], ACT.Abs)
         nc.scalar.activation(sgn[:], wgt_t[:], ACT.Sign, bias=TINY)
-        nc.scalar.activation(own2[:], own_t[:], ACT.Copy, scale=2.0)
         nc.scalar.activation(log_mag[:], mag[:], ACT.Ln, bias=TINY)
         warm_exp = pool.tile([P, 1], F32, name="warm_exp")
         nc.scalar.activation(warm_exp[:], log_mag[:, 0:1], ACT.Exp, scale=0.0)
+        own_cols = psum.tile([P, PACK, P], F32, name="own_cols", tag="dots3")
+        for j in range(PACK):
+            nc.tensor.transpose(own_cols[:, j, :], own_row[:, j::PACK], ident[:])
+        nc.scalar.activation(own2[:], own_cols[:, :, HALF_ROW], ACT.Copy, scale=2.0)
         for j in range(PACK):
             nc.scalar.activation(row2[:, j : j + 1], log_mag[:, j : j + 1], ACT.Identity, scale=2.0, bias=own2[:, j : j + 1])
 

@@ -69,7 +69,7 @@ def tile_picked_ykrr_bias_p_kernel(
         nc.sync.dma_start(own_row[HALF_ROW:, :], own.rearrange("t o -> o t"))
         nc.sync.dma_start(xw_win[:].bitcast(I32), x_words[0].rearrange("p n t -> p (n t)").bitcast(I32))
         for q in range(4):
-            nc.sync.dma_start(es_win[q::32, :].bitcast(I32), e_scales[0, q::4, :].bitcast(I32))
+            nc.sync.dma_start(es_win[32 * q : 32 * q + 4, :].bitcast(I32), e_scales[0, 4 * q : 4 * q + 4, :].bitcast(I32))
         nc.sync.dma_start(ew_win[:].bitcast(I32), e_words[0].rearrange("p n t -> p (n t)").bitcast(I32))
 
         nc.scalar.activation(
@@ -103,8 +103,11 @@ def tile_picked_ykrr_bias_p_kernel(
         for q in range(4):
             nc.sync.dma_start(xs_rows[32 * q : 32 * q + 4, :], xs_rows[X_ROW + 4 * q : X_ROW + 4 * q + 4, :])
         nc.vector.tensor_copy(xw_dealt[:].rearrange("p j m -> p m j"), xw_win[:].indirect(offs_t[:]))
-        es_picked = pool.tile([P, V], U8, name="es_picked", tag="picked_bytes", align_bytes=64)
-        nc.vector.tensor_copy(es_picked[:], es_win[:].indirect(qry_t[:]))
+        es_first = pool.tile([P, V // 2], U8, name="es_first", tag="picked_bytes", align_bytes=64)
+        es_second = pool.tile([P, V // 2], U8, name="es_second", align_bytes=64)
+        nc.vector.tensor_copy(es_first[:], es_win[:].indirect(qry_t[:, :16]))
+        nc.vector.tensor_copy(es_second[:], es_win[:].indirect(qry_t[:, 16:]))
+        es_picked = [es_first, es_second]
 
         spread = []
         for h, chunks in enumerate(([0], [1, 2, 3])):
@@ -117,6 +120,18 @@ def tile_picked_ykrr_bias_p_kernel(
             for n in range(len(chunks)):
                 nc.tensor.transpose(wide[:, n * P : (n + 1) * P], half_col[:, n : n + 1].to_broadcast([P, P]), ident[:])
             spread.append(wide)
+
+        warm = psum.tile([P, 2, V // 2], F32, name="warm", tag="turned1")
+        for n in range(2):
+            nc.tensor.matmul_mx(
+                out=warm[:, n, :],
+                lhsT=xw_dealt[:, n, :].bitcast(FP8X4),
+                lhsT_scale=es_first[:, :P],
+                rhs=xw_dealt[:].rearrange("p j m -> p (j m)")[:, : V // 2].bitcast(FP8X4),
+                rhs_scale=es_first[:],
+                start=True,
+                stop=True,
+            )
 
         norms2 = []
         for h in range(2):
@@ -152,7 +167,7 @@ def tile_picked_ykrr_bias_p_kernel(
                     lhsT=xw_dealt[:, j, :].bitcast(FP8X4),
                     lhsT_scale=xs_dealt[:, j, :],
                     rhs=ew_picked[h][:, lo : lo + CHUNK].bitcast(FP8X4),
-                    rhs_scale=es_picked[:, c * CHUNK : (c + 1) * CHUNK],
+                    rhs_scale=es_picked[h][:, lo : lo + CHUNK],
                     start=True,
                     stop=True,
                 )

@@ -57,7 +57,7 @@ def tile_picked_ykrr_bias_p_kernel(
             zero[:HALF_ROW, :].unsqueeze(1).to_broadcast([HALF_ROW, (W - FIRST_FILL) // 16, 16]),
         )
         xw_win = after_xw.tile([P, T], U32, name="xw_win", offset=0, align_bytes=64)
-        ident = held.tile([P, P], F32, name="ident", offset=0, align_bytes=64)
+        ident = pool.tile([P, P], F32, name="ident", align_bytes=64)
         ew_win = held.tile([P, W], U32, name="ew_win", offset=4 * P, align_bytes=64)
         make_identity(nc, ident[:])
 

@@ -24,6 +24,7 @@ SCALE_ROWS = 16
 X_ROW = P - SCALE_ROWS
 HALF_ROW = 127
 FIRST_FILL = 64
+FIRST_BANKS = ["dots0", "turned0", "spread0", "turned1"]
 TINY = 2.0 ** -64
 
 
@@ -81,10 +82,10 @@ def tile_picked_ykrr_bias_p_kernel(
         log_mag = pool.tile([P, PACK], F32, name="log_mag")
         row2 = pool.tile([P, PACK], F32, name="row2")
         nc.scalar.activation(mag[:], wgt_t[:], ACT.Abs)
-        nc.scalar.activation(sgn[:], wgt_t[:], ACT.Sign, bias=TINY)
         nc.scalar.activation(log_mag[:], mag[:], ACT.Ln, bias=TINY)
         warm_exp = pool.tile([P, 1], F32, name="warm_exp")
         nc.scalar.activation(warm_exp[:], log_mag[:, 0:1], ACT.Exp, scale=0.0)
+        nc.scalar.activation(sgn[:], wgt_t[:], ACT.Sign, bias=TINY)
         own_cols = psum.tile([P, PACK, P], F32, name="own_cols", tag="dots3")
         for j in range(PACK):
             nc.tensor.transpose(own_cols[:, j, :], own_row[:, j::PACK], ident[:])
@@ -159,11 +160,15 @@ def tile_picked_ykrr_bias_p_kernel(
 
         spans = []
         for c in range(V // CHUNK):
-            dots = psum.tile([P, PACK, CHUNK], F32, name=f"dots{c}")
+            if c == 0:
+                slots = [psum.tile([P, CHUNK], F32, name=f"first{j}", tag=tag) for j, tag in enumerate(FIRST_BANKS)]
+            else:
+                dots = psum.tile([P, PACK, CHUNK], F32, name=f"dots{c}")
+                slots = [dots[:, j, :] for j in range(PACK)]
             h, lo = divmod(c * CHUNK, V // 2)
             for j in range(PACK):
                 nc.tensor.matmul_mx(
-                    out=dots[:, j, :],
+                    out=slots[j][:],
                     lhsT=xw_dealt[:, j, :].bitcast(FP8X4),
                     lhsT_scale=xs_dealt[:, j, :],
                     rhs=ew_picked[h][:, lo : lo + CHUNK].bitcast(FP8X4),
@@ -171,25 +176,24 @@ def tile_picked_ykrr_bias_p_kernel(
                     start=True,
                     stop=True,
                 )
-            width = CHUNK if 0 < c < V // CHUNK - 1 else CHUNK // 2
+            width = CHUNK if c < V // CHUNK - 1 else CHUNK // 2
             for at in range(0, CHUNK, width):
                 first = c * CHUNK + at
-                terms = first if c == 0 else first - CHUNK
                 expo2 = pool.tile([P, PACK, width], F32, name=f"expo2_{first}", tag=f"expo_bytes{first}", align_bytes=64)
-                nc.vector.tensor_tensor(expo2[:], dots[:, :, at : at + width], norms2[min(c, 1)][:, :, terms : terms + width], ALU.add)
-                if c > 0 or at == 0:
-                    rounded = pool.tile([P, CHUNK if c == 0 else width, PACK], BF16, name=f"a_bf{first}", align_bytes=64)
-                into = rounded[:, at : at + width, :] if c == 0 else rounded[:]
+                if c == 0:
+                    for j in range(PACK):
+                        nc.vector.tensor_tensor(expo2[:, j, :], slots[j][:], norms2[0][:, j, :], ALU.add)
+                else:
+                    terms = first - CHUNK
+                    nc.vector.tensor_tensor(expo2[:], dots[:, :, at : at + width], norms2[1][:, :, terms : terms + width], ALU.add)
+                rounded = pool.tile([P, width, PACK], BF16, name=f"a_bf{first}", align_bytes=64)
                 nc.scalar.activation(
-                    into.rearrange("p (g i) j -> p g j i", i=4),
+                    rounded[:].rearrange("p (g i) j -> p g j i", i=4),
                     expo2[:].rearrange("p j (g i) -> p g j i", i=4),
                     ACT.Exp,
                     scale=0.5,
                 )
-                if c > 0:
-                    spans.append((first, width, rounded))
-                elif at > 0:
-                    spans.append((0, CHUNK, rounded))
+                spans.append((first, width, rounded))
 
         dual_codes = pool.tile([P, N], U32, name="dual_codes", tag="expo_bytes0", align_bytes=64)
         nc.vector.quantize_mx(out=dual_codes[:].bitcast(FP8X4), scales=dual_scales[:], in_=dual_bf[:].rearrange("p m j -> p (m j)"))

@@ -24,7 +24,8 @@ SCALE_ROWS = 16
 X_ROW = P - SCALE_ROWS
 HALF_ROW = 127
 FIRST_FILL = 64
-FIRST_BANKS = ["dots0", "turned0", "spread0", "turned1"]
+FIRST_BANKS = ["dots0", "turned0"]
+PIECE = CHUNK // 2
 TINY = 2.0 ** -64
 
 
@@ -84,7 +85,7 @@ def tile_picked_ykrr_bias_p_kernel(
         nc.scalar.activation(mag[:], wgt_t[:], ACT.Abs)
         nc.scalar.activation(log_mag[:], mag[:], ACT.Ln, bias=TINY)
         warm_exp = pool.tile([P, 1], F32, name="warm_exp")
-        nc.scalar.activation(warm_exp[:], log_mag[:, 0:1], ACT.Exp, scale=0.0)
+        nc.scalar.activation(warm_exp[:], mag[:, 0:1], ACT.Exp, scale=0.0)
         nc.scalar.activation(sgn[:], wgt_t[:], ACT.Sign, bias=TINY)
         own_cols = psum.tile([P, PACK, P], F32, name="own_cols", tag="dots3")
         for j in range(PACK):
@@ -127,9 +128,9 @@ def tile_picked_ykrr_bias_p_kernel(
             nc.tensor.matmul_mx(
                 out=warm[:, n, :],
                 lhsT=xw_dealt[:, n, :].bitcast(FP8X4),
-                lhsT_scale=es_first[:, :P],
+                lhsT_scale=es_second[:, :P],
                 rhs=xw_dealt[:].rearrange("p j m -> p (j m)")[:, : V // 2].bitcast(FP8X4),
-                rhs_scale=es_first[:],
+                rhs_scale=es_second[:],
                 start=True,
                 stop=True,
             )
@@ -160,15 +161,13 @@ def tile_picked_ykrr_bias_p_kernel(
 
         spans = []
         for c in range(V // CHUNK):
-            if c == 0:
-                slots = [psum.tile([P, CHUNK], F32, name=f"first{j}", tag=tag) for j, tag in enumerate(FIRST_BANKS)]
-            else:
-                dots = psum.tile([P, PACK, CHUNK], F32, name=f"dots{c}")
-                slots = [dots[:, j, :] for j in range(PACK)]
+            tags = FIRST_BANKS if c == 0 else [f"dots{c}"]
+            per_bank = PACK // len(tags)
+            banks = [psum.tile([P, per_bank, CHUNK], F32, name=f"dots{c}_{n}", tag=tag) for n, tag in enumerate(tags)]
             h, lo = divmod(c * CHUNK, V // 2)
             for j in range(PACK):
                 nc.tensor.matmul_mx(
-                    out=slots[j][:],
+                    out=banks[j // per_bank][:, j % per_bank, :],
                     lhsT=xw_dealt[:, j, :].bitcast(FP8X4),
                     lhsT_scale=xs_dealt[:, j, :],
                     rhs=ew_picked[h][:, lo : lo + CHUNK].bitcast(FP8X4),
@@ -176,24 +175,27 @@ def tile_picked_ykrr_bias_p_kernel(
                     start=True,
                     stop=True,
                 )
-            width = CHUNK if c < V // CHUNK - 1 else CHUNK // 2
-            for at in range(0, CHUNK, width):
+            last = c == V // CHUNK - 1
+            for at in range(0, CHUNK, PIECE):
                 first = c * CHUNK + at
-                expo2 = pool.tile([P, PACK, width], F32, name=f"expo2_{first}", tag=f"expo_bytes{first}", align_bytes=64)
-                if c == 0:
-                    for j in range(PACK):
-                        nc.vector.tensor_tensor(expo2[:, j, :], slots[j][:], norms2[0][:, j, :], ALU.add)
-                else:
-                    terms = first - CHUNK
-                    nc.vector.tensor_tensor(expo2[:], dots[:, :, at : at + width], norms2[1][:, :, terms : terms + width], ALU.add)
-                rounded = pool.tile([P, width, PACK], BF16, name=f"a_bf{first}", align_bytes=64)
+                terms = first if c == 0 else first - CHUNK
+                expo2 = pool.tile([P, PACK, PIECE], F32, name=f"expo2_{first}", tag=f"expo_bytes{first}", align_bytes=64)
+                for n, bank in enumerate(banks):
+                    slots = slice(n * per_bank, (n + 1) * per_bank)
+                    nc.vector.tensor_tensor(
+                        expo2[:, slots, :], bank[:, :, at : at + PIECE], norms2[min(c, 1)][:, slots, terms : terms + PIECE], ALU.add
+                    )
+                if last or at == 0:
+                    width = PIECE if last else CHUNK
+                    rounded = pool.tile([P, width, PACK], BF16, name=f"a_bf{first}", align_bytes=64)
+                    spans.append((first, width, rounded))
+                into = rounded[:] if last else rounded[:, at : at + PIECE, :]
                 nc.scalar.activation(
-                    rounded[:].rearrange("p (g i) j -> p g j i", i=4),
+                    into.rearrange("p (g i) j -> p g j i", i=4),
                     expo2[:].rearrange("p j (g i) -> p g j i", i=4),
                     ACT.Exp,
                     scale=0.5,
                 )
-                spans.append((first, width, rounded))
 
         dual_codes = pool.tile([P, N], U32, name="dual_codes", tag="expo_bytes0", align_bytes=64)
         nc.vector.quantize_mx(out=dual_codes[:].bitcast(FP8X4), scales=dual_scales[:], in_=dual_bf[:].rearrange("p m j -> p (m j)"))

@@ -24,8 +24,11 @@ SCALE_ROWS = 16
 X_ROW = P - SCALE_ROWS
 HALF_ROW = 127
 FIRST_FILL = 64
-FIRST_BANKS = ["dots0", "turned0"]
+LN_FILL = 192
+SECOND_BANKS = ["turned0", "turned1", "spread0", "spread1"]
 PIECE = CHUNK // 2
+GROUPS = ([0], [1], [2, 3])
+SPREAD_BANKS = ["spread0", "spread1", "dots2"]
 TINY = 2.0 ** -64
 
 
@@ -54,20 +57,21 @@ def tile_picked_ykrr_bias_p_kernel(
         nc.vector.memset(xs_win[:X_ROW, :].bitcast(I32), 0)
         nc.vector.tensor_copy(half_win[:HALF_ROW, :FIRST_FILL], zero[:HALF_ROW, 0:1].to_broadcast([HALF_ROW, FIRST_FILL]))
         nc.vector.memset(es_win[:].bitcast(I32), 0)
+        nc.gpsimd.memset(own_row[:HALF_ROW, LN_FILL:], 0.0)
         nc.vector.tensor_copy(
             half_win[:HALF_ROW, FIRST_FILL:W].rearrange("p (g i) -> p g i", i=16),
             zero[:HALF_ROW, :].unsqueeze(1).to_broadcast([HALF_ROW, (W - FIRST_FILL) // 16, 16]),
         )
         xw_win = after_xw.tile([P, T], U32, name="xw_win", offset=0, align_bytes=64)
-        ident = pool.tile([P, P], F32, name="ident", align_bytes=64)
+        ident = held.tile([P, P], F32, name="ident", offset=0, align_bytes=64)
         ew_win = held.tile([P, W], U32, name="ew_win", offset=4 * P, align_bytes=64)
         make_identity(nc, ident[:])
 
         nc.sync.dma_start(offs_t[:], offs)
         nc.scalar.dma_start(xs_win[X_ROW:, :].bitcast(I32), x_scales[0].bitcast(I32))
+        nc.sync.dma_start(wgt_t[:], wgt.rearrange("(p j) o -> p (j o)", j=PACK))
         nc.sync.dma_start(qry_t[:], qry)
         nc.scalar.dma_start(half_win[HALF_ROW : HALF_ROW + 1, :], half[0:1, :])
-        nc.sync.dma_start(wgt_t[:], wgt.rearrange("(p j) o -> p (j o)", j=PACK))
         nc.sync.dma_start(own_row[HALF_ROW:, :], own.rearrange("t o -> o t"))
         nc.sync.dma_start(xw_win[:].bitcast(I32), x_words[0].rearrange("p n t -> p (n t)").bitcast(I32))
         for q in range(4):
@@ -75,31 +79,28 @@ def tile_picked_ykrr_bias_p_kernel(
         nc.sync.dma_start(ew_win[:].bitcast(I32), e_words[0].rearrange("p n t -> p (n t)").bitcast(I32))
 
         nc.scalar.activation(
-            own_row[:HALF_ROW, :], half_win[:HALF_ROW, 0:1].to_broadcast([HALF_ROW, S]), ACT.Ln, bias=1.0
+            own_row[:HALF_ROW, :LN_FILL], half_win[:HALF_ROW, 0:1].to_broadcast([HALF_ROW, LN_FILL]), ACT.Ln, bias=1.0
         )
         mag = pool.tile([P, PACK], F32, name="mag")
         sgn = pool.tile([P, PACK], F32, name="sgn")
-        own2 = pool.tile([P, PACK], F32, name="own2")
         log_mag = pool.tile([P, PACK], F32, name="log_mag")
-        row2 = pool.tile([P, PACK], F32, name="row2")
         nc.scalar.activation(mag[:], wgt_t[:], ACT.Abs)
         nc.scalar.activation(log_mag[:], mag[:], ACT.Ln, bias=TINY)
         warm_exp = pool.tile([P, 1], F32, name="warm_exp")
         nc.scalar.activation(warm_exp[:], mag[:, 0:1], ACT.Exp, scale=0.0)
-        nc.scalar.activation(sgn[:], wgt_t[:], ACT.Sign, bias=TINY)
         own_cols = psum.tile([P, PACK, P], F32, name="own_cols", tag="dots3")
         for j in range(PACK):
             nc.tensor.transpose(own_cols[:, j, :], own_row[:, j::PACK], ident[:])
-        nc.scalar.activation(own2[:], own_cols[:, :, HALF_ROW], ACT.Copy, scale=2.0)
-        for j in range(PACK):
-            nc.scalar.activation(row2[:, j : j + 1], log_mag[:, j : j + 1], ACT.Identity, scale=2.0, bias=own2[:, j : j + 1])
 
         xs_picked = pool.tile([P, S], U8, name="xs_picked", tag="picked_bytes", align_bytes=64)
         xs_dealt = pool.tile([P, PACK, P], U8, name="xs_dealt", align_bytes=64)
-        half_picked = pool.tile([P, V], F32, name="half_picked", align_bytes=64)
         xw_dealt = pool.tile([P, PACK, P], U32, name="xw_dealt", align_bytes=64)
         nc.vector.tensor_copy(xs_picked[:], xs_win[:].indirect(offs_t[:]))
-        nc.vector.tensor_copy(half_picked[:], half_win[:].indirect(qry_t[:]))
+        half_picked = []
+        for h in range(2):
+            piece = pool.tile([P, V // 2], F32, name=f"half_picked{h}", align_bytes=64)
+            nc.vector.tensor_copy(piece[:], half_win[:].indirect(qry_t[:, h * 16 : (h + 1) * 16]))
+            half_picked.append(piece)
         nc.vector.tensor_copy(xs_dealt[:], xs_picked[:].rearrange("p (m j) -> p j m", j=PACK))
         xs_rows = xs_dealt[:].rearrange("p j m -> p (j m)").bitcast(I32)
         for q in range(4):
@@ -112,35 +113,29 @@ def tile_picked_ykrr_bias_p_kernel(
         es_picked = [es_first, es_second]
 
         spread = []
-        for h, chunks in enumerate(([0], [1, 2, 3])):
-            turned = psum.tile([P, len(chunks), P], F32, name=f"turned{h}")
+        for g, chunks in enumerate(GROUPS):
+            turned = psum.tile([P, len(chunks), P], F32, name=f"turned{g}", tag=f"turned{g % 2}")
             for n, c in enumerate(chunks):
-                nc.tensor.transpose(turned[:, n, :], half_picked[:, c * P : (c + 1) * P], ident[:])
-            half_col = pool.tile([P, len(chunks)], F32, name=f"half_col{h}")
-            nc.scalar.activation(half_col[:], turned[:, :, HALF_ROW], ACT.Copy, scale=-2.0)
-            wide = psum.tile([P, len(chunks) * P], F32, name=f"spread{h}")
+                nc.tensor.transpose(turned[:, n, :], half_picked[c // 2][:, c % 2 * P : (c % 2 + 1) * P], ident[:])
+            half_col = pool.tile([P, len(chunks)], F32, name=f"half_col{g}")
+            nc.scalar.activation(half_col[:], turned[:, :, HALF_ROW], ACT.Copy, scale=-1.0)
+            wide = psum.tile([P, len(chunks) * P], F32, name=f"spread{g}", tag=SPREAD_BANKS[g])
             for n in range(len(chunks)):
                 nc.tensor.transpose(wide[:, n * P : (n + 1) * P], half_col[:, n : n + 1].to_broadcast([P, P]), ident[:])
             spread.append(wide)
 
-        warm = psum.tile([P, 2, V // 2], F32, name="warm", tag="turned1")
-        for n in range(2):
-            nc.tensor.matmul_mx(
-                out=warm[:, n, :],
-                lhsT=xw_dealt[:, n, :].bitcast(FP8X4),
-                lhsT_scale=es_second[:, :P],
-                rhs=xw_dealt[:].rearrange("p j m -> p (j m)")[:, : V // 2].bitcast(FP8X4),
-                rhs_scale=es_second[:],
-                start=True,
-                stop=True,
-            )
-
+        row2 = pool.tile([P, PACK], F32, name="row2", tag="half_picked0", align_bytes=64)
+        for j in range(PACK):
+            nc.scalar.activation(row2[:, j : j + 1], own_cols[:, j, HALF_ROW:], ACT.Identity, bias=log_mag[:, j : j + 1])
         norms2 = []
-        for h in range(2):
-            piece = pool.tile([P, PACK, CHUNK if h == 0 else V - CHUNK], F32, name=f"norms2_{h}", align_bytes=64)
+        for g, chunks in enumerate(GROUPS):
+            piece = pool.tile([P, PACK, len(chunks) * CHUNK], F32, name=f"norms2_{g}", align_bytes=64)
             for j in range(PACK):
-                nc.scalar.activation(piece[:, j, :], spread[h][:], ACT.Identity, bias=row2[:, j : j + 1])
-            norms2.append(piece)
+                nc.scalar.activation(piece[:, j, :], spread[g][:], ACT.Identity, bias=row2[:, j : j + 1])
+            for n in range(len(chunks)):
+                norms2.append(piece[:, :, n * CHUNK : (n + 1) * CHUNK])
+
+        nc.scalar.activation(sgn[:], wgt_t[:], ACT.Sign, bias=TINY)
 
         dual_t = after_xw.tile([P, PACK, N], F32, name="dual_t", offset=0, align_bytes=64)
         nc.sync.dma_start(dual_t[:], dual.rearrange("(p j) m -> p j m", j=PACK))
@@ -161,7 +156,7 @@ def tile_picked_ykrr_bias_p_kernel(
 
         spans = []
         for c in range(V // CHUNK):
-            tags = FIRST_BANKS if c == 0 else [f"dots{c}"]
+            tags = [f"dots{c}", SECOND_BANKS[c]]
             per_bank = PACK // len(tags)
             banks = [psum.tile([P, per_bank, CHUNK], F32, name=f"dots{c}_{n}", tag=tag) for n, tag in enumerate(tags)]
             h, lo = divmod(c * CHUNK, V // 2)
@@ -176,15 +171,18 @@ def tile_picked_ykrr_bias_p_kernel(
                     stop=True,
                 )
             last = c == V // CHUNK - 1
+            expo = pool.tile([P, PACK, CHUNK], F32, name=f"expo{c}", tag=f"expo_bytes{c}", align_bytes=64)
+            nc.vector.scalar_tensor_tensor(expo[:, :per_bank, :], banks[0][:], 0.5, norms2[c][:, :per_bank, :], ALU.mult, ALU.add)
             for at in range(0, CHUNK, PIECE):
                 first = c * CHUNK + at
-                terms = first if c == 0 else first - CHUNK
-                expo2 = pool.tile([P, PACK, PIECE], F32, name=f"expo2_{first}", tag=f"expo_bytes{first}", align_bytes=64)
-                for n, bank in enumerate(banks):
-                    slots = slice(n * per_bank, (n + 1) * per_bank)
-                    nc.vector.tensor_tensor(
-                        expo2[:, slots, :], bank[:, :, at : at + PIECE], norms2[min(c, 1)][:, slots, terms : terms + PIECE], ALU.add
-                    )
+                nc.vector.scalar_tensor_tensor(
+                    expo[:, per_bank:, at : at + PIECE],
+                    banks[1][:, :, at : at + PIECE],
+                    0.5,
+                    norms2[c][:, per_bank:, at : at + PIECE],
+                    ALU.mult,
+                    ALU.add,
+                )
                 if last or at == 0:
                     width = PIECE if last else CHUNK
                     rounded = pool.tile([P, width, PACK], BF16, name=f"a_bf{first}", align_bytes=64)
@@ -192,9 +190,8 @@ def tile_picked_ykrr_bias_p_kernel(
                 into = rounded[:] if last else rounded[:, at : at + PIECE, :]
                 nc.scalar.activation(
                     into.rearrange("p (g i) j -> p g j i", i=4),
-                    expo2[:].rearrange("p j (g i) -> p g j i", i=4),
+                    expo[:, :, at : at + PIECE].rearrange("p j (g i) -> p g j i", i=4),
                     ACT.Exp,
-                    scale=0.5,
                 )
 
         dual_codes = pool.tile([P, N], U32, name="dual_codes", tag="expo_bytes0", align_bytes=64)
@@ -203,7 +200,7 @@ def tile_picked_ykrr_bias_p_kernel(
             a_codes = pool.tile([P, width], U32, name=f"a_codes{first}", align_bytes=64)
             a_scales = pool.tile([P, width], U8, name=f"a_scales{first}", align_bytes=64)
             nc.vector.quantize_mx(out=a_codes[:].bitcast(FP8X4), scales=a_scales[:], in_=rounded[:].rearrange("p v j -> p (v j)"))
-            acc = psum.tile([P, width], F32, name=f"acc{n}", tag=["turned0", "turned1", "spread0", "spread1", "dots0"][n])
+            acc = psum.tile([P, width], F32, name=f"acc{n}", tag=["dots0", "turned0", "dots1", "turned1", "dots2"][n])
             nc.tensor.matmul_mx(
                 out=acc[:],
                 lhsT=dual_codes[:].bitcast(FP8X4),

@@ -21,14 +21,12 @@ P = 128
 PACK = 4
 CHUNK = 128
 SCALE_ROWS = 16
-X_ROW = P - SCALE_ROWS
-HALF_ROW = 127
-FIRST_FILL = 64
+S_ROW = P - SCALE_ROWS
+LAST_ROW = 127
 LN_FILL = 192
-SECOND_BANKS = ["turned0", "turned1", "spread0", "spread1"]
+DOT_BANKS = (["turned1", "turned0"], ["dots0", "dots1"], ["dots2", "spread0"], ["dots3", "spread1"])
 PIECE = CHUNK // 2
-GROUPS = ([0], [1], [2, 3])
-SPREAD_BANKS = ["spread0", "spread1", "dots2"]
+WORD_PIECES = (128, 128, 256)
 TINY = 2.0 ** -64
 
 
@@ -39,102 +37,96 @@ def tile_picked_ykrr_bias_p_kernel(
     with ExitStack() as ctx:
         pool = ctx.enter_context(tc.tile_pool(name="keep", bufs=1))
         psum = ctx.enter_context(tc.psum_pool(name="psum", bufs=1))
-
         held = ctx.enter_context(tc.tile_pool(name="held", bufs=1))
-
         after_xw = ctx.enter_context(tc.tile_pool(name="after_xw", bufs=1))
+
         offs_t = pool.tile([P, S // 16], U16, name="offs_t")
         qry_t = pool.tile([P, V // 16], U16, name="qry_t")
-        xs_win = pool.tile([P, T], U8, name="xs_win", tag="xs_bytes", align_bytes=64)
-        es_win = pool.tile([P, W], U8, name="es_win", tag="es_bytes", align_bytes=64)
-        half_win = pool.tile([P, W], F32, name="half_win", tag="half_bytes", align_bytes=64)
-
+        xs_win = pool.tile([P, T], U8, name="xs_win", align_bytes=64)
+        es_win = pool.tile([P, W], U8, name="es_win", align_bytes=64)
+        half_win = pool.tile([P, W], F32, name="half_win", align_bytes=64)
         wgt_t = pool.tile([P, PACK], F32, name="wgt_t")
-        own_row = pool.tile([P, S], F32, name="own_row", align_bytes=64)
+        own_row = pool.tile([P, S], F32, name="own_row", tag="own_bytes", align_bytes=64)
 
+        planes = pool.tile([P, S + V], U8, name="planes", align_bytes=64)
+        nc.gpsimd.memset(planes[:].bitcast(I32), 0)
         zero = held.tile([P, 16], F32, name="zero", offset=4 * P - 32)
         nc.vector.memset(zero[:], 0.0)
-        nc.vector.memset(xs_win[:X_ROW, :].bitcast(I32), 0)
-        nc.vector.tensor_copy(half_win[:HALF_ROW, :FIRST_FILL], zero[:HALF_ROW, 0:1].to_broadcast([HALF_ROW, FIRST_FILL]))
-        nc.vector.memset(es_win[:].bitcast(I32), 0)
-        nc.gpsimd.memset(own_row[:HALF_ROW, LN_FILL:], 0.0)
+        nc.vector.memset(xs_win[:S_ROW, :].bitcast(I32), 0)
+        nc.vector.memset(es_win[:S_ROW, :].bitcast(I32), 0)
+        nc.gpsimd.memset(own_row[:LAST_ROW, LN_FILL:], 0.0)
         nc.vector.tensor_copy(
-            half_win[:HALF_ROW, FIRST_FILL:W].rearrange("p (g i) -> p g i", i=16),
-            zero[:HALF_ROW, :].unsqueeze(1).to_broadcast([HALF_ROW, (W - FIRST_FILL) // 16, 16]),
+            half_win[:LAST_ROW, :].rearrange("p (g i) -> p g i", i=16),
+            zero[:LAST_ROW, :].unsqueeze(1).to_broadcast([LAST_ROW, W // 16, 16]),
         )
         xw_win = after_xw.tile([P, T], U32, name="xw_win", offset=0, align_bytes=64)
         ident = held.tile([P, P], F32, name="ident", offset=0, align_bytes=64)
-        ew_win = held.tile([P, W], U32, name="ew_win", offset=4 * P, align_bytes=64)
+        ew_win = held.tile([P, W], U32, name="ew_win", offset=4 * P + 64, align_bytes=64)
         make_identity(nc, ident[:])
 
         nc.sync.dma_start(offs_t[:], offs)
-        nc.scalar.dma_start(xs_win[X_ROW:, :].bitcast(I32), x_scales[0].bitcast(I32))
-        nc.sync.dma_start(wgt_t[:], wgt.rearrange("(p j) o -> p (j o)", j=PACK))
+        nc.scalar.dma_start(xs_win[S_ROW:, :].bitcast(I32), x_scales[0].bitcast(I32))
         nc.sync.dma_start(qry_t[:], qry)
-        nc.scalar.dma_start(half_win[HALF_ROW : HALF_ROW + 1, :], half[0:1, :])
-        nc.sync.dma_start(own_row[HALF_ROW:, :], own.rearrange("t o -> o t"))
+        nc.scalar.dma_start(es_win[S_ROW:, :].bitcast(I32), e_scales[0].bitcast(I32))
+        nc.scalar.dma_start(half_win[LAST_ROW:, :], half[0:1, :])
+        nc.sync.dma_start(wgt_t[:], wgt.rearrange("(p j) o -> p (j o)", j=PACK))
         nc.sync.dma_start(xw_win[:].bitcast(I32), x_words[0].rearrange("p n t -> p (n t)").bitcast(I32))
-        for q in range(4):
-            nc.sync.dma_start(es_win[32 * q : 32 * q + 4, :].bitcast(I32), e_scales[0, 4 * q : 4 * q + 4, :].bitcast(I32))
-        nc.sync.dma_start(ew_win[:].bitcast(I32), e_words[0].rearrange("p n t -> p (n t)").bitcast(I32))
+        nc.scalar.dma_start(own_row[LAST_ROW:, :], own.rearrange("t o -> o t"))
 
         nc.scalar.activation(
-            own_row[:HALF_ROW, :LN_FILL], half_win[:HALF_ROW, 0:1].to_broadcast([HALF_ROW, LN_FILL]), ACT.Ln, bias=1.0
+            own_row[:LAST_ROW, :LN_FILL], own_row[:LAST_ROW, LN_FILL : LN_FILL + 1].to_broadcast([LAST_ROW, LN_FILL]), ACT.Ln, bias=1.0
         )
-        mag = pool.tile([P, PACK], F32, name="mag")
-        sgn = pool.tile([P, PACK], F32, name="sgn")
-        log_mag = pool.tile([P, PACK], F32, name="log_mag")
-        nc.scalar.activation(mag[:], wgt_t[:], ACT.Abs)
-        nc.scalar.activation(log_mag[:], mag[:], ACT.Ln, bias=TINY)
-        warm_exp = pool.tile([P, 1], F32, name="warm_exp")
-        nc.scalar.activation(warm_exp[:], mag[:, 0:1], ACT.Exp, scale=0.0)
-        own_cols = psum.tile([P, PACK, P], F32, name="own_cols", tag="dots3")
-        for j in range(PACK):
-            nc.tensor.transpose(own_cols[:, j, :], own_row[:, j::PACK], ident[:])
+        nc.sync.dma_start(ew_win[:].bitcast(I32), e_words[0].rearrange("p n t -> p (n t)").bitcast(I32))
 
-        xs_picked = pool.tile([P, S], U8, name="xs_picked", tag="picked_bytes", align_bytes=64)
-        xs_dealt = pool.tile([P, PACK, P], U8, name="xs_dealt", align_bytes=64)
-        xw_dealt = pool.tile([P, PACK, P], U32, name="xw_dealt", align_bytes=64)
-        nc.vector.tensor_copy(xs_picked[:], xs_win[:].indirect(offs_t[:]))
         half_picked = []
         for h in range(2):
             piece = pool.tile([P, V // 2], F32, name=f"half_picked{h}", align_bytes=64)
-            nc.vector.tensor_copy(piece[:], half_win[:].indirect(qry_t[:, h * 16 : (h + 1) * 16]))
+            nc.scalar.activation(piece[:], half_win[:].indirect(qry_t[:, h * 16 : (h + 1) * 16]), ACT.Copy)
             half_picked.append(piece)
-        nc.vector.tensor_copy(xs_dealt[:], xs_picked[:].rearrange("p (m j) -> p j m", j=PACK))
-        xs_rows = xs_dealt[:].rearrange("p j m -> p (j m)").bitcast(I32)
+
+        mag = pool.tile([P, PACK], F32, name="mag")
+        log_mag = pool.tile([P, PACK], F32, name="log_mag")
+        nc.scalar.activation(mag[:], wgt_t[:], ACT.Abs)
+        nc.scalar.activation(log_mag[:], mag[:], ACT.Ln, bias=TINY)
+
+        picked = pool.tile([P, S + V], U8, name="picked", align_bytes=64)
+        nc.vector.tensor_copy(picked[:, :S].rearrange("p (j m) -> p m j", j=PACK), xs_win[:].indirect(offs_t[:]))
+        nc.vector.tensor_copy(picked[:, S:], es_win[:].indirect(qry_t[:]))
         for q in range(4):
-            nc.sync.dma_start(xs_rows[32 * q : 32 * q + 4, :], xs_rows[X_ROW + 4 * q : X_ROW + 4 * q + 4, :])
+            nc.sync.dma_start(
+                planes[32 * q : 32 * q + 4, :].bitcast(I32), picked[S_ROW + 4 * q : S_ROW + 4 * q + 4, :].bitcast(I32)
+            )
+        xw_dealt = pool.tile([P, PACK, P], U32, name="xw_dealt", align_bytes=64)
         nc.vector.tensor_copy(xw_dealt[:].rearrange("p j m -> p m j"), xw_win[:].indirect(offs_t[:]))
-        es_first = pool.tile([P, V // 2], U8, name="es_first", tag="picked_bytes", align_bytes=64)
-        es_second = pool.tile([P, V // 2], U8, name="es_second", align_bytes=64)
-        nc.vector.tensor_copy(es_first[:], es_win[:].indirect(qry_t[:, :16]))
-        nc.vector.tensor_copy(es_second[:], es_win[:].indirect(qry_t[:, 16:]))
-        es_picked = [es_first, es_second]
 
-        spread = []
-        for g, chunks in enumerate(GROUPS):
-            turned = psum.tile([P, len(chunks), P], F32, name=f"turned{g}", tag=f"turned{g % 2}")
-            for n, c in enumerate(chunks):
-                nc.tensor.transpose(turned[:, n, :], half_picked[c // 2][:, c % 2 * P : (c % 2 + 1) * P], ident[:])
-            half_col = pool.tile([P, len(chunks)], F32, name=f"half_col{g}")
-            nc.scalar.activation(half_col[:], turned[:, :, HALF_ROW], ACT.Copy, scale=-1.0)
-            wide = psum.tile([P, len(chunks) * P], F32, name=f"spread{g}", tag=SPREAD_BANKS[g])
-            for n in range(len(chunks)):
+        wides = []
+        for h in range(2):
+            turned = psum.tile([P, 2, P], F32, name=f"turned{h}", tag=f"turned{h}")
+            for n in range(2):
+                nc.tensor.transpose(turned[:, n, :], half_picked[h][:, n * P : (n + 1) * P], ident[:])
+            half_col = pool.tile([P, 2], F32, name=f"half_col{h}")
+            nc.scalar.activation(half_col[:], turned[:, :, LAST_ROW], ACT.Copy, scale=-2.0)
+            wide = psum.tile([P, 2 * P], F32, name=f"spread{h}", tag=f"spread{h}")
+            for n in range(2):
                 nc.tensor.transpose(wide[:, n * P : (n + 1) * P], half_col[:, n : n + 1].to_broadcast([P, P]), ident[:])
-            spread.append(wide)
-
-        row2 = pool.tile([P, PACK], F32, name="row2", tag="half_picked0", align_bytes=64)
+            wides.append(wide)
+        own_cols = psum.tile([P, PACK, P], F32, name="own_cols", tag="turned1")
         for j in range(PACK):
-            nc.scalar.activation(row2[:, j : j + 1], own_cols[:, j, HALF_ROW:], ACT.Identity, bias=log_mag[:, j : j + 1])
-        norms2 = []
-        for g, chunks in enumerate(GROUPS):
-            piece = pool.tile([P, PACK, len(chunks) * CHUNK], F32, name=f"norms2_{g}", align_bytes=64)
-            for j in range(PACK):
-                nc.scalar.activation(piece[:, j, :], spread[g][:], ACT.Identity, bias=row2[:, j : j + 1])
-            for n in range(len(chunks)):
-                norms2.append(piece[:, :, n * CHUNK : (n + 1) * CHUNK])
-
+            nc.tensor.transpose(own_cols[:, j, :], own_row[:, j::PACK], ident[:])
+        warm_exp = pool.tile([P, 1], F32, name="warm_exp")
+        nc.scalar.activation(warm_exp[:], half_col[:, 0:1], ACT.Exp, scale=0.0, bias=log_mag[:, 0:1])
+        own_t = pool.tile([P, PACK], F32, name="own_t")
+        nc.scalar.activation(own_t[:], own_cols[:, :, LAST_ROW], ACT.Copy)
+        row = pool.tile([P, PACK], F32, name="row", tag="row_bytes")
+        row2 = pool.tile([P, PACK], F32, name="row2")
+        nc.gpsimd.tensor_tensor(row[:], own_t[:], log_mag[:], ALU.add)
+        nc.gpsimd.tensor_scalar(row2[:], row[:], 2.0, 0.0, ALU.mult, ALU.add)
+        half2 = []
+        for h in range(2):
+            piece = pool.tile([P, V // 2], F32, name=f"half2_{h}", align_bytes=64)
+            nc.scalar.activation(piece[:], wides[h][:], ACT.Copy)
+            half2.append(piece)
+        sgn = pool.tile([P, PACK], F32, name="sgn", tag="row_bytes")
         nc.scalar.activation(sgn[:], wgt_t[:], ACT.Sign, bias=TINY)
 
         dual_t = after_xw.tile([P, PACK, N], F32, name="dual_t", offset=0, align_bytes=64)
@@ -143,55 +135,54 @@ def tile_picked_ykrr_bias_p_kernel(
         nc.sync.dma_start(bias_t[:], bias)
         dual_scales = pool.tile([P, N], U8, name="dual_scales", align_bytes=64)
 
-        ew_picked = []
-        for h in range(2):
-            piece = pool.tile([P, V // 2], U32, name=f"ew_picked{h}", align_bytes=64)
-            nc.vector.tensor_copy(piece[:], ew_win[:].indirect(qry_t[:, h * 16 : (h + 1) * 16]))
-            ew_picked.append(piece)
+        ew_picked = pool.tile([P, V], U32, name="ew_picked", tag="own_bytes", align_bytes=64)
+        first = 0
+        for width in WORD_PIECES:
+            nc.vector.tensor_copy(ew_picked[:, first : first + width], ew_win[:].indirect(qry_t[:, first // 16 : (first + width) // 16]))
+            first = first + width
 
-        dual_bf = held.tile([P, N, PACK], BF16, name="dual_bf", offset=4 * P, align_bytes=64)
+        dual_bf = held.tile([P, N, PACK], BF16, name="dual_bf", offset=4 * P + 64, align_bytes=64)
         nc.gpsimd.tensor_tensor(
             dual_bf[:], dual_t[:].rearrange("p j m -> p m j"), sgn[:].unsqueeze(1).to_broadcast([P, N, PACK]), ALU.mult
         )
 
         spans = []
         for c in range(V // CHUNK):
-            tags = [f"dots{c}", SECOND_BANKS[c]]
+            tags = DOT_BANKS[c]
             per_bank = PACK // len(tags)
             banks = [psum.tile([P, per_bank, CHUNK], F32, name=f"dots{c}_{n}", tag=tag) for n, tag in enumerate(tags)]
-            h, lo = divmod(c * CHUNK, V // 2)
             for j in range(PACK):
                 nc.tensor.matmul_mx(
                     out=banks[j // per_bank][:, j % per_bank, :],
                     lhsT=xw_dealt[:, j, :].bitcast(FP8X4),
-                    lhsT_scale=xs_dealt[:, j, :],
-                    rhs=ew_picked[h][:, lo : lo + CHUNK].bitcast(FP8X4),
-                    rhs_scale=es_picked[h][:, lo : lo + CHUNK],
+                    lhsT_scale=planes[:, j * P : (j + 1) * P],
+                    rhs=ew_picked[:, c * CHUNK : (c + 1) * CHUNK].bitcast(FP8X4),
+                    rhs_scale=planes[:, S + c * CHUNK : S + (c + 1) * CHUNK],
                     start=True,
                     stop=True,
                 )
             last = c == V // CHUNK - 1
             expo = pool.tile([P, PACK, CHUNK], F32, name=f"expo{c}", tag=f"expo_bytes{c}", align_bytes=64)
-            nc.vector.scalar_tensor_tensor(expo[:, :per_bank, :], banks[0][:], 0.5, norms2[c][:, :per_bank, :], ALU.mult, ALU.add)
-            for at in range(0, CHUNK, PIECE):
-                first = c * CHUNK + at
+            h, lo = divmod(c * CHUNK, V // 2)
+            for j in range(PACK):
                 nc.vector.scalar_tensor_tensor(
-                    expo[:, per_bank:, at : at + PIECE],
-                    banks[1][:, :, at : at + PIECE],
-                    0.5,
-                    norms2[c][:, per_bank:, at : at + PIECE],
-                    ALU.mult,
+                    expo[:, j, :],
+                    banks[j // per_bank][:, j % per_bank, :],
+                    row2[:, j : j + 1],
+                    half2[h][:, lo : lo + CHUNK],
+                    ALU.add,
                     ALU.add,
                 )
-                if last or at == 0:
-                    width = PIECE if last else CHUNK
-                    rounded = pool.tile([P, width, PACK], BF16, name=f"a_bf{first}", align_bytes=64)
-                    spans.append((first, width, rounded))
-                into = rounded[:] if last else rounded[:, at : at + PIECE, :]
+            width = PIECE if last else CHUNK
+            for at in range(0, CHUNK, width):
+                first = c * CHUNK + at
+                rounded = pool.tile([P, width, PACK], BF16, name=f"a_bf{first}", align_bytes=64)
+                spans.append((first, width, rounded))
                 nc.scalar.activation(
-                    into.rearrange("p (g i) j -> p g j i", i=4),
-                    expo[:, :, at : at + PIECE].rearrange("p j (g i) -> p g j i", i=4),
+                    rounded[:].rearrange("p (g i) j -> p g j i", i=4),
+                    expo[:, :, at : at + width].rearrange("p j (g i) -> p g j i", i=4),
                     ACT.Exp,
+                    scale=0.5,
                 )
 
         dual_codes = pool.tile([P, N], U32, name="dual_codes", tag="expo_bytes0", align_bytes=64)
@@ -200,7 +191,7 @@ def tile_picked_ykrr_bias_p_kernel(
             a_codes = pool.tile([P, width], U32, name=f"a_codes{first}", align_bytes=64)
             a_scales = pool.tile([P, width], U8, name=f"a_scales{first}", align_bytes=64)
             nc.vector.quantize_mx(out=a_codes[:].bitcast(FP8X4), scales=a_scales[:], in_=rounded[:].rearrange("p v j -> p (v j)"))
-            acc = psum.tile([P, width], F32, name=f"acc{n}", tag=["dots0", "turned0", "dots1", "turned1", "dots2"][n])
+            acc = psum.tile([P, width], F32, name=f"acc{n}", tag=["turned1", "turned0", "dots0", "dots1", "dots2"][n])
             nc.tensor.matmul_mx(
                 out=acc[:],
                 lhsT=dual_codes[:].bitcast(FP8X4),

@@ -88,6 +88,8 @@ def tile_picked_ykrr_bias_p_kernel(
         log_mag = pool.tile([P, PACK], F32, name="log_mag")
         nc.scalar.activation(mag[:], wgt_t[:], ACT.Abs)
         nc.scalar.activation(log_mag[:], mag[:], ACT.Ln, bias=TINY)
+        log_mag2 = pool.tile([P, PACK], F32, name="log_mag2")
+        nc.gpsimd.tensor_scalar(log_mag2[:], log_mag[:], 2.0, 0.0, ALU.mult, ALU.add)
 
         picked = pool.tile([P, S + V], U8, name="picked", align_bytes=64)
         nc.vector.tensor_copy(picked[:, :S].rearrange("p (j m) -> p m j", j=PACK), xs_win[:].indirect(offs_t[:]))
@@ -115,18 +117,15 @@ def tile_picked_ykrr_bias_p_kernel(
             nc.tensor.transpose(own_cols[:, j, :], own_row[:, j::PACK], ident[:])
         warm_exp = pool.tile([P, 1], F32, name="warm_exp")
         nc.scalar.activation(warm_exp[:], half_col[:, 0:1], ACT.Exp, scale=0.0, bias=log_mag[:, 0:1])
-        own_t = pool.tile([P, PACK], F32, name="own_t")
-        nc.scalar.activation(own_t[:], own_cols[:, :, LAST_ROW], ACT.Copy)
-        row = pool.tile([P, PACK], F32, name="row", tag="row_bytes")
         row2 = pool.tile([P, PACK], F32, name="row2")
-        nc.gpsimd.tensor_tensor(row[:], own_t[:], log_mag[:], ALU.add)
-        nc.gpsimd.tensor_scalar(row2[:], row[:], 2.0, 0.0, ALU.mult, ALU.add)
+        for j in range(PACK):
+            nc.scalar.activation(row2[:, j : j + 1], own_cols[:, j, LAST_ROW:], ACT.Identity, scale=2.0, bias=log_mag2[:, j : j + 1])
         half2 = []
         for h in range(2):
             piece = pool.tile([P, V // 2], F32, name=f"half2_{h}", align_bytes=64)
             nc.scalar.activation(piece[:], wides[h][:], ACT.Copy)
             half2.append(piece)
-        sgn = pool.tile([P, PACK], F32, name="sgn", tag="row_bytes")
+        sgn = pool.tile([P, PACK], F32, name="sgn")
         nc.scalar.activation(sgn[:], wgt_t[:], ACT.Sign, bias=TINY)
 
         dual_t = after_xw.tile([P, PACK, N], F32, name="dual_t", offset=0, align_bytes=64)

from contextlib import ExitStack

import concourse.mybir as mybir
from concourse.masks import make_identity

K, T, S, N, V, W = 512, 2048, 512, 128, 512, 2048
FLOPS = 2 * K * S * V + 2 * S * N * V
BYTES = 2 * (K * T + K * T // 32) + 4 * (W + 2 * S + S * N + N + N * V) + 2 * 128 * (S + V) // 16

F32 = mybir.dt.float32
BF16 = mybir.dt.bfloat16
I32 = mybir.dt.int32
U32 = mybir.dt.uint32
U16 = mybir.dt.uint16
U8 = mybir.dt.uint8
FP8X4 = mybir.dt.float8_e4m3fn_x4
ACT = mybir.ActivationFunctionType
ALU = mybir.AluOpType

P = 128
PACK = 4
CHUNK = 128
SCALE_ROWS = 16
S_ROW = P - SCALE_ROWS
LAST_ROW = 127
LN_FILL = 192
DOT_BANKS = (["turned1", "turned0"], ["dots0", "dots1"], ["dots2", "spread0"], ["dots3", "spread1"])
PIECE = CHUNK // 2
WORD_PIECES = (128, 128, 256)
TINY = 2.0 ** -64


def tile_picked_ykrr_bias_p_kernel(
    tc, x_words, x_scales, e_words, e_scales, half, own, wgt, dual, bias, offs, qry, out
):
    nc = tc.nc
    with ExitStack() as ctx:
        pool = ctx.enter_context(tc.tile_pool(name="keep", bufs=1))
        psum = ctx.enter_context(tc.psum_pool(name="psum", bufs=1))
        held = ctx.enter_context(tc.tile_pool(name="held", bufs=1))
        after_xw = ctx.enter_context(tc.tile_pool(name="after_xw", bufs=1))

        offs_t = pool.tile([P, S // 16], U16, name="offs_t")
        qry_t = pool.tile([P, V // 16], U16, name="qry_t")
        xs_win = pool.tile([P, T], U8, name="xs_win", align_bytes=64)
        es_win = pool.tile([P, W], U8, name="es_win", align_bytes=64)
        half_win = pool.tile([P, W], F32, name="half_win", align_bytes=64)
        wgt_t = pool.tile([P, PACK], F32, name="wgt_t")
        own_row = pool.tile([P, S], F32, name="own_row", tag="own_bytes", align_bytes=64)

        planes = pool.tile([P, S + V], U8, name="planes", align_bytes=64)
        nc.gpsimd.memset(planes[:].bitcast(I32), 0)
        zero = held.tile([P, 16], F32, name="zero", offset=4 * P - 32)
        nc.vector.memset(zero[:], 0.0)
        nc.vector.memset(xs_win[:S_ROW, :].bitcast(I32), 0)
        nc.vector.memset(es_win[:S_ROW, :].bitcast(I32), 0)
        nc.gpsimd.memset(own_row[:LAST_ROW, LN_FILL:], 0.0)
        nc.vector.tensor_copy(
            half_win[:LAST_ROW, :].rearrange("p (g i) -> p g i", i=16),
            zero[:LAST_ROW, :].unsqueeze(1).to_broadcast([LAST_ROW, W // 16, 16]),
        )
        xw_win = after_xw.tile([P, T], U32, name="xw_win", offset=0, align_bytes=64)
        ident = held.tile([P, P], F32, name="ident", offset=0, align_bytes=64)
        ew_win = held.tile([P, W], U32, name="ew_win", offset=4 * P + 64, align_bytes=64)
        make_identity(nc, ident[:])

        nc.sync.dma_start(offs_t[:], offs)
        nc.scalar.dma_start(xs_win[S_ROW:, :].bitcast(I32), x_scales[0].bitcast(I32))
        nc.sync.dma_start(qry_t[:], qry)
        nc.scalar.dma_start(es_win[S_ROW:, :].bitcast(I32), e_scales[0].bitcast(I32))
        nc.scalar.dma_start(half_win[LAST_ROW:, :], half[0:1, :])
        nc.sync.dma_start(wgt_t[:], wgt.rearrange("(p j) o -> p (j o)", j=PACK))
        nc.sync.dma_start(xw_win[:].bitcast(I32), x_words[0].rearrange("p n t -> p (n t)").bitcast(I32))
        nc.scalar.dma_start(own_row[LAST_ROW:, :], own.rearrange("t o -> o t"))

        nc.scalar.activation(
            own_row[:LAST_ROW, :LN_FILL], own_row[:LAST_ROW, LN_FILL : LN_FILL + 1].to_broadcast([LAST_ROW, LN_FILL]), ACT.Ln, bias=1.0
        )
        nc.sync.dma_start(ew_win[:].bitcast(I32), e_words[0].rearrange("p n t -> p (n t)").bitcast(I32))

        half_picked = []
        for h in range(2):
            piece = pool.tile([P, V // 2], F32, name=f"half_picked{h}", align_bytes=64)
            nc.scalar.activation(piece[:], half_win[:].indirect(qry_t[:, h * 16 : (h + 1) * 16]), ACT.Copy)
            half_picked.append(piece)

        mag = pool.tile([P, PACK], F32, name="mag")
        log_mag = pool.tile([P, PACK], F32, name="log_mag")
        nc.scalar.activation(mag[:], wgt_t[:], ACT.Abs)
        nc.scalar.activation(log_mag[:], mag[:], ACT.Ln, bias=TINY)
        log_mag2 = pool.tile([P, PACK], F32, name="log_mag2")
        nc.gpsimd.tensor_scalar(log_mag2[:], log_mag[:], 2.0, 0.0, ALU.mult, ALU.add)

        picked = pool.tile([P, S + V], U8, name="picked", align_bytes=64)
        nc.vector.tensor_copy(picked[:, :S].rearrange("p (j m) -> p m j", j=PACK), xs_win[:].indirect(offs_t[:]))
        nc.vector.tensor_copy(picked[:, S:], es_win[:].indirect(qry_t[:]))
        for q in range(4):
            nc.sync.dma_start(
                planes[32 * q : 32 * q + 4, :].bitcast(I32), picked[S_ROW + 4 * q : S_ROW + 4 * q + 4, :].bitcast(I32)
            )
        xw_dealt = pool.tile([P, PACK, P], U32, name="xw_dealt", align_bytes=64)
        nc.vector.tensor_copy(xw_dealt[:].rearrange("p j m -> p m j"), xw_win[:].indirect(offs_t[:]))

        wides = []
        for h in range(2):
            turned = psum.tile([P, 2, P], F32, name=f"turned{h}", tag=f"turned{h}")
            for n in range(2):
                nc.tensor.transpose(turned[:, n, :], half_picked[h][:, n * P : (n + 1) * P], ident[:])
            half_col = pool.tile([P, 2], F32, name=f"half_col{h}")
            nc.scalar.activation(half_col[:], turned[:, :, LAST_ROW], ACT.Copy, scale=-2.0)
            wide = psum.tile([P, 2 * P], F32, name=f"spread{h}", tag=f"spread{h}")
            for n in range(2):
                nc.tensor.transpose(wide[:, n * P : (n + 1) * P], half_col[:, n : n + 1].to_broadcast([P, P]), ident[:])
            wides.append(wide)
        own_cols = psum.tile([P, PACK, P], F32, name="own_cols", tag="turned1")
        for j in range(PACK):
            nc.tensor.transpose(own_cols[:, j, :], own_row[:, j::PACK], ident[:])
        warm_exp = pool.tile([P, 1], F32, name="warm_exp")
        nc.scalar.activation(warm_exp[:], half_col[:, 0:1], ACT.Exp, scale=0.0, bias=log_mag[:, 0:1])
        row2 = pool.tile([P, PACK], F32, name="row2")
        for j in range(PACK):
            nc.scalar.activation(row2[:, j : j + 1], own_cols[:, j, LAST_ROW:], ACT.Identity, scale=2.0, bias=log_mag2[:, j : j + 1])
        half2 = []
        for h in range(2):
            piece = pool.tile([P, V // 2], F32, name=f"half2_{h}", align_bytes=64)
            nc.scalar.activation(piece[:], wides[h][:], ACT.Copy)
            half2.append(piece)
        sgn = pool.tile([P, PACK], F32, name="sgn")
        nc.scalar.activation(sgn[:], wgt_t[:], ACT.Sign, bias=TINY)

        dual_t = after_xw.tile([P, PACK, N], F32, name="dual_t", offset=0, align_bytes=64)
        nc.sync.dma_start(dual_t[:], dual.rearrange("(p j) m -> p j m", j=PACK))
        bias_t = after_xw.tile([P, 1], F32, name="bias_t", offset=4 * PACK * N, align_bytes=64)
        nc.sync.dma_start(bias_t[:], bias)
        dual_scales = pool.tile([P, N], U8, name="dual_scales", align_bytes=64)

        ew_picked = pool.tile([P, V], U32, name="ew_picked", tag="own_bytes", align_bytes=64)
        first = 0
        for width in WORD_PIECES:
            nc.vector.tensor_copy(ew_picked[:, first : first + width], ew_win[:].indirect(qry_t[:, first // 16 : (first + width) // 16]))
            first = first + width

        dual_bf = held.tile([P, N, PACK], BF16, name="dual_bf", offset=4 * P + 64, align_bytes=64)
        nc.gpsimd.tensor_tensor(
            dual_bf[:], dual_t[:].rearrange("p j m -> p m j"), sgn[:].unsqueeze(1).to_broadcast([P, N, PACK]), ALU.mult
        )

        spans = []
        for c in range(V // CHUNK):
            tags = DOT_BANKS[c]
            per_bank = PACK // len(tags)
            banks = [psum.tile([P, per_bank, CHUNK], F32, name=f"dots{c}_{n}", tag=tag) for n, tag in enumerate(tags)]
            for j in range(PACK):
                nc.tensor.matmul_mx(
                    out=banks[j // per_bank][:, j % per_bank, :],
                    lhsT=xw_dealt[:, j, :].bitcast(FP8X4),
                    lhsT_scale=planes[:, j * P : (j + 1) * P],
                    rhs=ew_picked[:, c * CHUNK : (c + 1) * CHUNK].bitcast(FP8X4),
                    rhs_scale=planes[:, S + c * CHUNK : S + (c + 1) * CHUNK],
                    start=True,
                    stop=True,
                )
            last = c == V // CHUNK - 1
            expo = pool.tile([P, PACK, CHUNK], F32, name=f"expo{c}", tag=f"expo_bytes{c}", align_bytes=64)
            h, lo = divmod(c * CHUNK, V // 2)
            for j in range(PACK):
                nc.vector.scalar_tensor_tensor(
                    expo[:, j, :],
                    banks[j // per_bank][:, j % per_bank, :],
                    row2[:, j : j + 1],
                    half2[h][:, lo : lo + CHUNK],
                    ALU.add,
                    ALU.add,
                )
            width = PIECE if last else CHUNK
            for at in range(0, CHUNK, width):
                first = c * CHUNK + at
                rounded = pool.tile([P, width, PACK], BF16, name=f"a_bf{first}", align_bytes=64)
                spans.append((first, width, rounded))
                nc.scalar.activation(
                    rounded[:].rearrange("p (g i) j -> p g j i", i=4),
                    expo[:, :, at : at + width].rearrange("p j (g i) -> p g j i", i=4),
                    ACT.Exp,
                    scale=0.5,
                )

        dual_codes = pool.tile([P, N], U32, name="dual_codes", tag="expo_bytes0", align_bytes=64)
        nc.vector.quantize_mx(out=dual_codes[:].bitcast(FP8X4), scales=dual_scales[:], in_=dual_bf[:].rearrange("p m j -> p (m j)"))
        for n, (first, width, rounded) in enumerate(spans):
            a_codes = pool.tile([P, width], U32, name=f"a_codes{first}", align_bytes=64)
            a_scales = pool.tile([P, width], U8, name=f"a_scales{first}", align_bytes=64)
            nc.vector.quantize_mx(out=a_codes[:].bitcast(FP8X4), scales=a_scales[:], in_=rounded[:].rearrange("p v j -> p (v j)"))
            acc = psum.tile([P, width], F32, name=f"acc{n}", tag=["turned1", "turned0", "dots0", "dots1", "dots2"][n])
            nc.tensor.matmul_mx(
                out=acc[:],
                lhsT=dual_codes[:].bitcast(FP8X4),
                lhsT_scale=dual_scales[:],
                rhs=a_codes[:].bitcast(FP8X4),
                rhs_scale=a_scales[:],
                start=True,
                stop=True,
            )
            result = pool.tile([P, width], F32, name=f"result{first}", align_bytes=64)
            nc.scalar.activation(result[:], acc[:], ACT.Tanh, bias=bias_t[:])
            nc.sync.dma_start(out[:, first : first + width], result[:])
